import numpy as np, ml_dtypes
CORES = [36,164,52,180,100,228,116,244]
N = 8
BF = ml_dtypes.bfloat16
def gentries(a):
    return np.ascontiguousarray(a.reshape(8, 16, -1).transpose(0, 2, 1)).reshape(8, -1)
def gtable(e):
    e = np.asarray(e); return np.ascontiguousarray(e.reshape(8, -1, 16).transpose(0, 2, 1)).reshape(128, -1).astype(np.int32)
I, V, G, M, RO = 896, 449, 64, 1024, 3
def grow(J):
    T = J.shape[0]; ar = np.arange(T); ch = np.zeros((T, 2 * I), np.int64); free = np.zeros((T, I + 1), np.int64); free[:, 1] = 1
    for t in range(1, I):
        j = J[:, t]; ch[ar, free[ar, j]] = t; free[ar, j] = 2 * t; free[:, t + 1] = 2 * t + 1
    ch[ar[:, None], free] = I + np.arange(I + 1)[None, :]
    return ch.reshape(T, I, 2)
def trees(rng, kind, lab):
    T = N * 8; k = kind.reshape(T, 1); t = np.arange(I)[None, :]; r = rng.random((T, I))
    level = t + 1 - 2 ** (np.frexp((t + 1).astype(np.float64))[1].astype(np.int64) - 1)
    J = np.where(k == 0, (r * (t + 1)).astype(np.int64), np.where(k == 1, t - np.minimum((4 * r).astype(np.int64), t), np.where(k == 2, t, level)))
    ch = grow(J); b = lab.reshape(T, 1); s = np.arange(I + 1)[None, :]
    pi = np.where(b == 0, np.argsort(rng.random((T, I)), axis=1), np.where(b == 1, t, I - 1 - t))
    lf = I + np.where(b == 0, np.argsort(rng.random((T, I + 1)), axis=1), np.where(b == 1, s, I - s))
    c = np.take_along_axis(np.concatenate([pi, lf], axis=1), ch.reshape(T, 2 * I), 1).reshape(T, I, 2)
    c = np.where(rng.random((T, I, 1)) < 0.5, c[:, :, ::-1], c)
    o = np.zeros_like(c); o[np.arange(T)[:, None], pi] = c
    return o[:, :, 0].reshape(N, 8, I), o[:, :, 1].reshape(N, 8, I)
def parts(rng):
    size = rng.random((N, 8, 1, I + V)); size[..., :I] = 0.4 + 0.6 * size[..., :I]
    h = np.minimum((256 * size * rng.random((N, 8, 16, I + V))).astype(np.int64), 255)
    return h, rng.integers(-50, 51, (N, 8, 16, V)), rng.integers(0, V, (N, 8, N - 1, G))
def pack(h, v, tr, s):
    return {"h0": np.ascontiguousarray(h.reshape(N, 128, I + V)).astype(np.int32), "vel": np.ascontiguousarray(v.reshape(N, 128, V)).astype(np.int32),
            "kl": np.stack([gtable(a) for a in tr[0]]), "kr": np.stack([gtable(a) for a in tr[1]]), "sl": np.stack([gtable(a.reshape(8, -1)) for a in s])}
def setup_inputs(rng):
    h, v, s = parts(rng)
    return pack(h, v, trees(rng, rng.integers(0, 2, (N, 8)), np.zeros((N, 8), np.int64)), s)
def setup_inputs_ties(rng):
    h, v, s = parts(rng)
    h[:, ::2] = 8 * rng.integers(0, 4, (N, 4, 1, I + V)); h[:, ::2, :, :I] += 16
    v[:, ::2] = 8 * rng.integers(-1, 2, (N, 4, 1, V))
    h[:, 1::2] = 100 + (rng.random((N, 4, 16, I + V)) < 0.0625); v[:, 1::2] = rng.integers(-1, 2, (N, 4, 1, V))
    return pack(h, v, trees(rng, rng.integers(0, 4, (N, 8)), rng.integers(0, 3, (N, 8))), s)
def setup_inputs_chain(rng):
    h, v, s = parts(rng)
    kind = np.tile(np.array([2, 3, 2, 1, 2, 3, 2, 0]), (N, 1)); lab = rng.integers(0, 3, (N, 8)); lab[:, 0] = np.arange(N) % 3; lab[:, 4] = (np.arange(N) + 1) % 3
    for g in (0, 4): h[:, g, :, :I] = 255; h[:, g, :, I:] = 0
    lab[:, 2] = 1 + np.arange(N) % 2; node = np.arange(I)[None, :]
    depth = np.where(lab[:, 2:3] == 1, node, I - 1 - node)
    h[:, 2, :, :I] = rng.integers(0, 128, (N, 16, I)) + 128 * (depth % 2)[:, None, :]; h[:, 2, :, I:] = 0
    return pack(h, v, trees(rng, kind, lab), s)
def setup_inputs_edge(rng):
    h, v, s = parts(rng)
    h = 255 * (rng.random(h.shape) < rng.random((N, 8, 1, I + V))).astype(np.int64); h[:, 3, :, :I] = 255; h[:, 3, :, I:] = 0
    v = 127 * rng.integers(-1, 2, v.shape); s[:, ::2] = (V - 1) * rng.integers(0, 2, (N, 4, N - 1, G))
    lab = rng.integers(1, 3, (N, 8)); lab[:, 0] = 1; lab[:, 1] = 2
    tr = trees(rng, rng.integers(0, 4, (N, 8)), lab)
    c = np.stack([tr[0][0, 0], tr[1][0, 0]], axis=1)
    w = int(c[0][c[0] != 1][0]); low = np.concatenate([np.array([w]), c[1], c[w:w + 1].reshape(-1)]); low = low[low < I + V]
    h[0, 0][:, low] = 0; h[0, 0][:, 1] = 255
    return pack(h, v, tr, s)
def setup_inputs_alike(rng):
    h, v, s = parts(rng); kl, kr = trees(rng, np.zeros((N, 8), np.int64), np.zeros((N, 8), np.int64))
    kl[:] = kl[:, :1]; kr[:] = kr[:, :1]
    g = rng.permutation(8); h[:, g[0], :, :I] = 0; h[:, g[1:3]] = h[:, g[1:3], :1]
    s = rng.choice(np.array([0, V - 1, V // 2, 3]), s.shape)
    return pack(h, v, (kl, kr), s)
def setup_inputs_spread(rng):
    h, v, s = parts(rng)
    h = np.minimum((np.exp2(1 + 8 * rng.random((N, 8, 1, I + V))) * rng.random(h.shape)).astype(np.int64), 255)
    v = np.minimum((np.exp2(7 * rng.random((N, 8, 1, V))) * rng.random(v.shape)).astype(np.int64), 127) * (2 * rng.integers(0, 2, v.shape) - 1)
    return pack(h, v, trees(rng, rng.integers(0, 4, (N, 8)), np.zeros((N, 8), np.int64)), s)
def check_inputs(d):
    bad = []
    for k, lo, hi in (("h0", 0, 255), ("vel", -127, 127), ("kl", 0, 2 * I), ("kr", 0, 2 * I), ("sl", 0, V - 1)):
        if np.min(d[k]) < lo or np.max(d[k]) > hi: bad.append("range of " + k)
    if bad: return bad
    for q in range(N):
        c = np.concatenate([gentries(d["kl"][q]), gentries(d["kr"][q])], axis=1).astype(np.int64); o = np.sort(c, axis=1)
        if np.any(o[:, 1:] == o[:, :-1]):
            bad.append("children all differ"); break
        up = np.tile(np.arange(2 * I + 1), (8, 1)); np.put_along_axis(up, c, np.tile(np.arange(I), (8, 2)), 1)
        for i in range(13): up = np.take_along_axis(up, up, 1)
        if np.any(up != up[:, :1]):
            bad.append("one tree"); break
    return bad
def reference(h0, vel, kl, kr, sl):
    E = 2 * I + 1; at = np.arange(I)
    H = np.zeros((N, 8, 16, E), np.int64); H[..., :I + V] = h0.reshape(N, 8, 16, I + V)
    v = vel.astype(np.int64).reshape(N, 8, 16, V); s = np.stack([gentries(a) for a in sl]).astype(np.int64).reshape(N, 8, N - 1, G)
    K = np.stack([np.stack([gentries(kl[q]), gentries(kr[q])], axis=1) for q in range(N)]).astype(np.int64)
    for rnd in range(RO):
        for q in range(N):
            for d in range(1, N):
                o = (q - d) % N; j = I + V + (d - 1) * G
                H[q, :, :, j:j + G] = np.take_along_axis(H[o, :, :, I:I + V], s[o, :, d - 1][:, None, :], 2)
        hc = [np.take_along_axis(H, K[:, :, a][:, :, None, :], 3) for a in (0, 1)]
        best = np.zeros((N, 8, I), np.int64); ca = np.zeros_like(best); cb = np.zeros_like(best)
        for a in (0, 1):
            inner = K[:, :, a] < I; u = np.where(inner, K[:, :, a], 0); su = np.add.reduce(hc[a], axis=2)
            for b in (0, 1):
                z = np.take_along_axis(K[:, :, 1 - b], u, 2)
                gain = su - np.add.reduce(np.maximum(hc[1 - a], np.take_along_axis(H, z[:, :, None, :], 3)), axis=2)
                more = inner & (gain > best); best = np.where(more, gain, best); ca = np.where(more, a, ca); cb = np.where(more, b, cb)
        key = np.full((N, 8, E + 1), -1, np.int64); key[..., :I] = np.where(best > 0, M * best + at, -1)
        par = np.full((N, 8, E), E, np.int64)
        for a in (0, 1): np.put_along_axis(par, K[:, :, a], np.tile(at, (N, 8, 1)), 2)
        near = np.take_along_axis(key, par[..., :I], 2)
        for a in (0, 1): near = np.maximum(near, np.take_along_axis(key, K[:, :, a], 2))
        q, g, n = np.nonzero(key[..., :I] > near); a = ca[q, g, n]; b = cb[q, g, n]
        u = K[q, g, a, n]; w = K[q, g, 1 - a, n]; x = K[q, g, b, u]
        K[q, g, 1 - a, n] = x; K[q, g, b, u] = w
        new = np.maximum(np.take_along_axis(H, K[:, :, 0][:, :, None, :], 3), np.take_along_axis(H, K[:, :, 1][:, :, None, :], 3))
        H[..., I:I + V] = np.minimum(np.maximum(H[..., I:I + V] + v, 0), 255); H[..., :I] = new
    return {"yh": H[..., :I + V].reshape(N, 128, I + V).astype(np.float32), "yk": K.reshape(N, 8, 2 * I).astype(np.float32)}

@@ -1,0 +1,465 @@
+from concourse.bass import DstId, RemoteDMATransfer
+from concourse.mybir import AluOpType, ActivationFunctionType, AxisListType
+
+A, F = AluOpType, ActivationFunctionType
+NI, NV, NG, RO = 896, 449, 64, 3
+SH = 7
+TW = 1808
+GH = NI + NV + SH
+NO = 2 * NI + 1
+UP = 112
+KL, KR, PP, SB, PA, IDB, ID = 1, 3, 5, 7, 9, 14, 15
+IC = 11
+CH = [(0, 192), (192, 512), (512, 704), (704, 896)]
+CQ = [(0, 224), (224, 448), (448, 672), (672, 896)]
+BK = [(0, 512), (512, 896)]
+F32, F16, B16 = "float32", "float16", "bfloat16"
+
+SCRATCH = {"kks": ("sbuf", [128, 2, 56], "int32"), "lst": ("sbuf", [128, 6, 56], "uint16"), "slu": ("sbuf", [128, 28], "uint16"),
+           "UB": ("sbuf", [128, 8, 16, 8], F16), "ZX": ("sbuf", [128, 65, 8], F16), "ZY": ("sbuf", [128, 49, 8], F16),
+           "ZS": ("sbuf", [128, 65, 8], F16), "WP": ("sbuf", [128, 2, 2, UP], F16), "Ih3": ("sbuf", [128, 8, 16], F16),
+           "sW": ("sbuf", [128, 2, 16], F32), "crow": ("sbuf", [128, 8, 16], B16), "pS": ("psum", [128, 8, 8, 8], F32)}
+for _dt, _bufs in (("int32", dict(h0s=1352, vels=452, sls=28, pi=128)),
+                   (B16, dict(velb=456, H0=TW, H1=TW, H2=TW, sb0=448, sb1=448, sb2=448, AA=NI, BB=NI, M0=NI, M1=NI, UPT=TW, UU=TW,
+                              U2=NI, DD=NI, N1=NI, one=512, Ib=128, Bp=128, Bn=128, sGp=32, sGn=32, zero=528, rows=256)),
+                   (F32, dict(LZ=452, H3=1348, vals=NI, W1=TW, W2=TW, RR=NI, T0=TW, TT=NI, KK=912, K2=NI, KP=NI, NT=912, NP=NI,
+                              EQ=256, EY=192, onef=64, cw=16, sK=64, sP=24, sN=48, iv=64, bt=24, bias=2)),
+                   (F16, dict(Ih=128, In1=128, In2=128))):
+    for _k in _bufs:
+        SCRATCH[_k] = ("sbuf", [128, _bufs[_k]], _dt)
+for _k in ("pD0", "pD1", "pF0", "pF1", "pX", "pY", "pW"):
+    SCRATCH[_k] = ("psum", [128, 512], F32)
+SEMAPHORES = ["cV", "cS", "cP", "cG", "dsl", "dlf", "dkl", "dkr", "dhi", "dve", "arr0", "arr1", "arr2", "sent",
+              "o0", "o1", "o2", "o3", "o4", "o5"]
+
+
+def rank_program(g, core, T, topo):
+    rank = T.rank_of(core)
+    if rank is None:
+        return
+    N = len(T.cores)
+    Q = {"V": g.vector, "S": g.scalar, "P": g.tensor, "G": g, "Y": g.sync}
+    cnt = {"V": 0, "S": 0, "P": 0, "G": 0}
+    seen = {e: {} for e in Q}
+    wr, rd, top = {}, {}, {}
+
+    def need(e, tok):
+        if seen[e].get(tok[0], 0) < tok[1]:
+            Q[e].wait_ge(T.sem[tok[0]], tok[1])
+            seen[e][tok[0]] = tok[1]
+
+    def order(e, r, w):
+        own = "c" + e
+        toks = {}
+        for k in r:
+            if k in wr:
+                toks[wr[k][0]] = max(toks.get(wr[k][0], 0), wr[k][1])
+        for k in w:
+            for t in rd.get(k, []) + ([wr[k]] if k in wr else []):
+                if t[0] != own:
+                    toks[t[0]] = max(toks.get(t[0], 0), t[1])
+        for s in toks:
+            need(e, (s, toks[s]))
+
+    def note(tok, r, w):
+        top[tok[0]] = tok[1]
+        for k in r:
+            rd.setdefault(k, []).append(tok)
+        for k in w:
+            wr[k] = tok
+            rd[k] = []
+
+    def op(e, fns, r, w):
+        order(e, r, w)
+        if not isinstance(fns, list):
+            fns = [fns]
+        for f in fns:
+            ins = f()
+        cnt[e] += 1
+        ins.then_inc(T.sem["c" + e], 1)
+        note(("c" + e, cnt[e]), r, w)
+
+    def dma(e, sem, out, in_, r, w):
+        order(e, r, w)
+        Q[e].dma_start(out, in_).then_inc(T.sem[sem], 16)
+        note((sem, top.get(sem, 0) + 16), r, w)
+
+    V, S, P = g.vector, g.scalar, g.tensor
+    H = [T.H0, T.H1, T.H2, T.H3]
+    pD, pF = [T.pD0, T.pD1], [T.pF0, T.pF1]
+    LK = {KL: 0, KR: 1, PP: 2, SB: 3, PA: 4, IC: 5}
+    ZK = {KL: 0, KR: 1, PA: 2, IC: 3}
+    I1, J1, J2 = T.Ih[0:UP, 0:UP], T.In1[0:UP, 0:UP], T.In2[0:UP, 0:UP]
+
+    def vc(out, in_, r, w):
+        op("V", lambda: V.tensor_copy(out, in_), r, w)
+
+    def vt(out, a, b, o, r, w):
+        op("V", lambda: V.tensor_tensor(out, a, b, o), r, w)
+
+    def vs(out, a, s, o, r, w):
+        op("V", lambda: V.tensor_scalar(out, a, s, None, o), r, w)
+
+    def sc(out, in_, r, w):
+        op("S", lambda: S.activation(out, in_, F.Copy), r, w)
+
+    def four(k):
+        return ["%s%d" % (k, c) for c in range(4)]
+
+    def lst(t, a=0, b=NI):
+        return T.lst[:, LK[t], a // 16:b // 16]
+
+    def ub(t):
+        return T.UB[0:UP, :, t, :]
+
+    def fld(ps, f, n=1):
+        return ps[0:UP, 64 * f:64 * (f + n)]
+
+    def zf(Z, f, n=1):
+        return Z[0:UP, 16 * f + 1:16 * (f + n):2, :]
+
+    def hkeys(t):
+        return four("H%d_" % t) + ["H%dl" % t, "H%dg" % t, "H%dp" % t]
+
+    def mm(out, lhsT, rhs, start=False, stop=False):
+        return lambda: P.matmul(out, lhsT, rhs, start, stop)
+
+    def const(ps, f, v, start=False):
+        a = {-1: 0, 0: 64, 1: 192}[v]
+        return mm(fld(ps, f), T.one[0:1, 0:UP], T.rows[0:1, a:a + 64], start)
+
+    def wrap(tab, off, rhs, ps, f0, nf, stop=False, start=False):
+        return [mm(ps[0:UP, 64 * f0 + r:64 * (f0 + nf):8], tab[:, off + r:off + NI:8], rhs, start and r == 0, stop and r == 7)
+                for r in range(8)]
+
+    def unwrap(ps, b, start=False, stop=False):
+        a, e = BK[b]
+        return [mm(ps[:, r:e - a:8], T.UB[0:UP, :, :, r], T.Ih[0:UP, a // 8:e // 8], start, stop) for r in range(8)]
+
+    def tolist(j, Z, f, stop=False, start=False):
+        return [mm(T.pW[:, 56 * j:56 * j + 56], Z[0:UP, 16 * f + 1 - h:16 * f + 17 - h, :], T.Ih[0:UP, h:UP:2],
+                   start and h == 0, stop and h == 1) for h in range(2)]
+
+    def fill(out, n, val, r, w):
+        op("G", lambda: g.iota(out, [[0, n]], val, 0, allow_small_or_imprecise_dtypes=True), r, w)
+
+    def pick(out, src, pat, t, keys):
+        op("G", lambda: g.affine_select(out, src, pat, A.is_equal, 0.0, -t, 1), ["one", "onef", "cw"], keys)
+
+    def put(out, src, pat, t, val, keys):
+        op("G", lambda: g.affine_select(out, src, pat, A.not_equal, val, -t, 1), keys + ["zero"], keys)
+
+    def twin(out, src, n, r, w):
+        op("G", lambda: g.affine_select(out, src, [[0, n]], A.is_ge, 0.0, 0, 0), [r], [w])
+
+    def send(t):
+        trs = []
+        for d in range(1, N):
+            dst = T.cores[(rank + d) % N]
+            rid, pid = topo.addr(dst, core)
+            trs.append(RemoteDMATransfer(dst_ids=[DstId(rid=rid, pnc=pid)], dma_engine_mask=1 << topo.engines(core, dst)[d - 1],
+                                         remote_sem=T.sem["arr%d" % t], src=T["sb%d" % t][:, NG * (d - 1):NG * d],
+                                         dst=H[t][:, GH + NG * (d - 1):GH + NG * d]))
+        order("G", ["sb%d" % t], [])
+        g.remote_dma_fused(trs, local_sem=T.sem.sent)
+        top["sent"] = top.get("sent", 0) + N - 1
+
+    def leaves(t, ps, key):
+        op("P", [mm(ps[:, 0:NV], T.Ib[:], H[t][:, NI + SH:GH], True, False), mm(ps[:, 0:NV], T.Ib[:], T.velb[:, 0:NV], False, True)],
+           ["Ib", "H%dl" % t, "velb"], [key])
+        out = T.H3[:, NI:NI + NV] if t == RO - 1 else H[t + 1][:, NI + SH:GH]
+        return [lambda: op("S", lambda: S.activation(T.LZ[:, 0:NV], ps[:, 0:NV], F.Relu, bias=255.0, scale=-1.0), [], [key, "LZ"]),
+                lambda: op("S", lambda: S.activation(out, T.LZ[:, 0:NV], F.Relu, bias=255.0, scale=-1.0), ["LZ"], ["H%dl" % (t + 1)])]
+
+    def ghosts(t):
+        sc(T["sb%d" % t][:], H[t][:, NI:GH].indirect(T.slu[:]), ["slu", "H%dl" % t, "H%d_3" % t], ["sb%d" % t])
+
+    for t in range(RO):
+        wr["H%dg" % t] = ("arr%d" % t, N - 1)
+        top["arr%d" % t] = N - 1
+
+    dma("Y", "dkl", T.kks[:, 0, :], T.kl[:], [], ["kk0"])
+    dma("S", "dkr", T.kks[:, 1, :], T.kr[:], [], ["kk1"])
+    dma("Y", "dlf", T.h0s[:, NI:GH], T.h0[:, NI - SH:NI + NV], [], ["h0l"])
+    dma("S", "dsl", T.sls[:], T.sl[:], [], ["sls"])
+    dma("Y", "dve", T.vels[:, 0:NV], T.vel[:], [], ["vels"])
+    dma("Y", "dhi", T.h0s[:, SH:NI], T.h0[:, 0:NI - SH], [], ["h0i"])
+
+    op("V", lambda: V.memset(T.zero[:], 0.0), [], ["zero"])
+    op("V", lambda: V.memset(T.one[:], 1.0), [], ["one"])
+    op("G", lambda: g.iota(T.iv[:], [[0, 8], [1, 8]], 0, 8, allow_small_or_imprecise_dtypes=True), [], ["iv"])
+    op("G", lambda: g.affine_select(T.Ib[:], T.one[:, 0:128], [[-1, 128]], A.is_equal, 0.0, 0, 1), ["one"], ["Ib"])
+    fill(T.W2[:, 0:904], 904, 0, [], ["W2"])
+    op("S", lambda: S.activation(T.W1[:, 0:512], T.zero[:, 0:512], F.Silu), ["zero"], ["W1"])
+    op("S", lambda: S.activation(T.W1[:, 512:904], T.zero[:, 0:392], F.Silu), ["zero"], ["W1"])
+    vc(T.WP[:], T.zero[:, 0:448], ["zero"], ["WP"])
+    for j in range(2):
+        vc(T.UB[:, 4 * j:4 * j + 4], T.zero[:, 0:512], ["zero"], ["UB"])
+    vc(T.Ih[:], T.Ib[:], ["Ib"], ["Ih"])
+    vc(T.Ih3[:], T.Ib[:], ["Ib"], ["Ih3"])
+    vc(ub(ID), T.iv[0:UP], ["iv", "UB"], ["u15"])
+    vc(T.ZS[:], T.zero[:, 0:520], ["zero"], ["ZS"])
+    op("V", lambda: V.memset(T.onef[:], 1.0), [], ["onef"])
+    op("V", lambda: V.memset(T.cw[:], -1.0 / 32), [], ["cw"])
+
+    for h in range(2):
+        vc(T.WP[:, :, h, h:UP:2], T.kks[:], ["kk0", "kk1", "WP"], ["WP%d" % h])
+    op("P", [mm(T.pS[0:UP, :, j, :], T.WP[:, j, h, :], T.Ih3[:, :, 8 * h:8 * h + 8], j + h == 0, j + h == 2) for j in range(2) for h in range(2)],
+       ["WP0", "WP1", "Ih3"], ["pS"])
+    vs(T.slu[:], T.sls[:], SH, A.add, ["sls"], ["slu"])
+    vs(T.lst[:, 0:2, :], T.kks[:], SH, A.add, ["kk0", "kk1"], ["l1", "l3"])
+    vc(T.UB[0:UP, :, KL:KR + 1:2, :], T.pS[0:UP, :, 0:2, :], ["UB"], ["pS", "u1", "u3"])
+    op("P", unwrap(pF[0], 0, True, True), ["UB", "u1", "u3", "u15", "Ih"], ["pF0"])
+    op("P", unwrap(pF[1], 1, True, True), ["UB", "u1", "u3", "u15", "Ih"], ["pF1"])
+    vc(T.sb0[:], T.h0s[:, NI:GH].indirect(T.slu[:]), ["slu", "h0l"], ["sb0"])
+    send(0)
+    for b in range(2):
+        a, e = BK[b]
+        op("S", lambda: S.activation(T.vals[:, a:e], pF[b][:, 0:e - a], F.Identity, bias=32.0 * NO, scale=-32.0), [], ["pF%d" % b, "vals%d" % b])
+    op("S", lambda: S.activation(T.W2[:].indirect(lst(KR)), T.vals[:], F.Silu), ["vals0", "vals1", "l3", "W2"], ["W2"])
+    vc(T.H0[:, NI + SH:GH], T.h0s[:, NI + SH:GH], ["h0l"], ["H0l"])
+    vc(T.velb[:, 0:NV], T.vels[:, 0:NV], ["vels"], ["velb"])
+    for f in leaves(0, T.pY, "pY"):
+        f()
+    vc(T.W1[:].indirect(lst(KL)), T.vals[:], ["vals0", "vals1", "l1", "W1"], ["W1"])
+
+    G8 = [[-16, 8]]
+    pick(T.sW[:, 0, 0:8], T.cw[:, 0:8], G8, KR, ["sW0"])
+    pick(T.sW[:, 0, 8:16], T.cw[:, 0:8], G8, ID, ["sW0"])
+    pick(T.sW[:, 1, 0:8], T.cw[:, 0:8], G8, KL, ["sW1"])
+    pick(T.sW[:, 1, 8:16], T.cw[:, 0:8], G8, ID, ["sW1"])
+    fill(T.H1[:, NI:NI + SH], SH, 0, [], ["H1_3"])
+    fill(T.Bp[:], 128, 4096, [], ["Bp"])
+    op("G", lambda: g.affine_select(T.Bp[:], T.Bp[:], [[-16, 8], [0, 16]], A.is_ge, 0.0, 0, 1), ["Bp"], ["Bp"])
+    op("G", lambda: g.affine_select(T.Bp[:], T.Bp[:], [[16, 8], [0, 16]], A.is_ge, 0.0, 15, -1), ["Bp"], ["Bp"])
+    fill(T.H0[:, 0:SH], SH, 0, [], ["H0p"])
+    fill(T.H0[:, TW - 8:TW], 8, 0, [], ["H0p"])
+    fill(T.crow[:], 128, -4096, [], ["crow"])
+    fill(T.crow[:, :, PA], 8, -2048, ["crow"], ["crow"])
+    pick(T.bt[:, 0:8], T.onef[:, 0:8], G8, IDB, ["bt"])
+    pick(T.bt[:, 8:16], T.onef[:, 0:8], G8, PA, ["bt"])
+
+    op("P", wrap(T.W2, SH, T.sW[:, 1, :], T.pX, 0, 2, False, True), ["W2", "sW1"], ["pX"])
+    op("P", wrap(T.W1, SH, T.sW[:, 0, :], T.pX, 0, 2, True), ["W1", "sW0"], ["pX"])
+    vc(T.H0[:, SH:SH + NI], T.h0s[:, SH:SH + NI], ["h0i", "h0l"], four("H0_"))
+    vs(T.Bn[:], T.Bp[:], -1.0, A.mult, ["Bp"], ["Bn"])
+    op("V", lambda: V.tensor_scalar(ub(IDB), T.iv[0:UP], 2.0, 1.0, A.mult, A.add), ["iv", "UB"], ["u14"])
+    vs(T.pi[0:UP, 0:64], fld(T.pX, 0), float(NO), A.add, [], ["pX", "pi0"])
+    op("V", lambda: V.tensor_scalar(T.pi[0:UP, 64:128], fld(T.pX, 1), float(NO), float(NI), A.add, A.min), [], ["pX", "pi1"])
+    vc(zf(T.ZS, ZK[KL]), T.pi[0:UP, 0:64], ["pi0", "ZS"], ["z0"])
+    op("P", tolist(0, T.ZS, ZK[KL], True, True), ["z0", "ZS"], ["pW"])
+    vc(ub(SB), T.pi[0:UP, 0:64], ["pi0", "UB"], ["u7"])
+    vc(ub(PA), T.pi[0:UP, 64:128], ["pi1", "UB"], ["u9"])
+    vc(zf(T.ZS, ZK[PA]), T.pi[0:UP, 64:128], ["pi1", "ZS"], ["z2"])
+    vs(lst(SB), T.pW[:, 0:56], SH, A.add, [], ["pW", "l7"])
+    vt(zf(T.ZS, ZK[IC]), ub(KL), ub(KR), A.min, ["u1", "u3", "ZS"], ["z3"])
+    op("V", lambda: V.tensor_reduce(T.bias[:, 0:1], T.bt[:, 0:8], AxisListType.X, A.add, negate=True), ["bt"], ["bias0"])
+    op("V", lambda: V.tensor_reduce(T.bt[:, 16:17], T.bt[:, 8:16], AxisListType.X, A.add), ["bt"], ["bt8"])
+
+    def late():
+        for j in range(2):
+            vc(zf(T.ZS, j), ub((KL, KR)[j]), ["u1", "u3", "ZS"], ["z%d" % j])
+        vs(T.In1[:], T.Ib[:], -1.0, A.mult, ["Ib"], ["In1"])
+        vs(T.In2[:], T.Ib[:], -2.0, A.mult, ["Ib"], ["In2"])
+        op("V", lambda: V.tensor_scalar(T.bias[:, 1:2], T.bt[:, 16:17], -2048.0, 2048.0, A.mult, A.add), ["bt8"], ["bias1"])
+
+    ghosts(1)
+    for j in range(2):
+        sc(T.UU[:, NI + 456 * j:NI + 456 * j + 456], T.zero[:, 0:456], ["zero"], ["UUp"])
+    fill(T.T0[:, NI:TW], TW - NI, -4096, [], ["T0t"])
+    fill(T.T0[:, 0:SH], SH, 0, [], ["T0t"])
+    send(1)
+    op("G", lambda: g.iota(T.rows[:], [[1, 2], [1, 2], [0, 64]], -1, 0, allow_small_or_imprecise_dtypes=True), [], ["rows"])
+    fill(T.H2[:, NI:NI + SH], SH, 0, [], ["H2_3"])
+    fill(T.KK[:, 0:SH], SH, 0, [], ["KKp"])
+    fill(T.KK[:, SH + NI:912], 912 - SH - NI, 0, [], ["KKp"])
+    fill(T.UPT[:, NI:TW], TW - NI, 0, [], ["UPp"])
+    fill(T.UPT[:, 0:SH], SH, 0, [], ["UPp"])
+    pick(T.sK[:, 0:32], T.onef[:, 0:32], [[0, 4]] + G8, IDB, ["sK"])
+    pick(T.sK[:, 32:64], T.onef[:, 0:32], [[0, 2], [-2, 2]] + G8, KL, ["sK"])
+    put(T.sK[:], T.sK[:], [[0, 8]] + G8, 0, -1.0, ["sK"])
+    put(T.sGp[:], T.zero[:, 0:32], [[0, 4]] + G8, PA, 4096.0, ["sGp"])
+    put(T.sGn[:], T.zero[:, 0:32], [[0, 4]] + G8, PA, -4096.0, ["sGn"])
+    pick(T.sP[:, 0:16], T.onef[:, 0:16], [[0, 2]] + G8, IDB, ["sP"])
+    pick(T.sP[:, 16:24], T.onef[:, 0:8], G8, ID, ["sP"])
+    put(T.sP[:], T.sP[:], [[0, 3]] + G8, 0, -1.0, ["sP"])
+    fill(T.UU[:, 0:SH], SH, 0, [], ["UUq"])
+
+    def last_fills():
+        pick(T.sN[:, 0:16], T.onef[:, 0:16], [[-2, 2]] + G8, KL, ["sN"])
+        pick(T.sN[:, 16:32], T.onef[:, 0:16], [[2, 2]] + G8, KR, ["sN"])
+        pick(T.sN[:, 32:48], T.onef[:, 0:16], [[0, 2]] + G8, PA, ["sN"])
+        put(T.sN[:, 32:40], T.sN[:, 32:40], G8, PA, -1.0, ["sN"])
+        fill(T.NT[:, 0:SH], SH, 0, [], ["NTp"])
+        fill(T.NT[:, SH + NI:912], 912 - SH - NI, NI, [], ["NTp"])
+        for k in (1, 2):
+            fill(H[k][:, 0:SH], SH, 0, [], ["H%dp" % k])
+            fill(H[k][:, TW - 8:TW], 8, 0, [], ["H%dp" % k])
+
+    uk = ["UB", "u1", "u3", "u5", "u7", "u9", "u14", "u15"]
+    for t in range(RO):
+        last = t == RO - 1
+        Ht, hk = H[t], hkeys(t)
+        win = Ht[:]
+        for b in range(2):
+            a, e = BK[b]
+            op("P", mm(pD[b][:, 0:e - a], T.crow[0:1], T.one[0:1, 0:e - a], True, False), ["crow"], ["pD%d" % b])
+        for b in range(2):
+            a, e = BK[b]
+            op("P", mm(pD[b][:, 0:e - a], T.Bp[:], Ht[:, SH + a:SH + e]), ["Bp"] + hk[0:4], ["pD%d" % b])
+        for b in range(2):
+            op("P", unwrap(pD[b], b), uk, ["pD%d" % b])
+        op("P", tolist(0, T.ZS, ZK[PA], False, True) + tolist(1, T.ZS, ZK[IC], True), ["z2", "z3"], ["pW"])
+        for c in range(4):
+            a, e = CH[c]
+            sc(T.AA[:, a:e], win.indirect(lst(SB, a, e)), hk + ["l7"], ["A%d" % c])
+        if t == 0:
+            late()
+        lv = [] if last else leaves(t + 1, T.pX, "pX")
+        for f in lv[0:1]:
+            f()
+        for c in range(4):
+            a, e = CH[c]
+            b = c // 2
+            o = BK[b][0]
+            vt(T.M0[:, a:e], win.indirect(lst(KR, a, e)), T.AA[:, a:e], A.max, hk + ["l3", "A%d" % c], ["M0%d" % c])
+            vt(T.M1[:, a:e], win.indirect(lst(KL, a, e)), T.AA[:, a:e], A.max, hk + ["l1", "A%d" % c], ["M1%d" % c])
+            op("P", [mm(pD[b][:, a - o:e - o], T.Bn[:], T.M0[:, a:e], False, c % 2 == 1),
+                     mm(pF[b][:, a - o:e - o], T.Bp[:], T.M0[:, a:e], True, False)], ["Bn", "Bp", "M0%d" % c], ["pD%d" % b, "pF%d" % b])
+            op("P", mm(pF[b][:, a - o:e - o], T.Bn[:], T.M1[:, a:e], False, True), ["M1%d" % c], ["pF%d" % b])
+            if c % 2 == 1:
+                op("S", lambda: S.activation(T.RR[:, o:e], pF[b][:, 0:e - o], F.Relu, bias=T.bias[:, 0:1]), ["bias0"], ["pF%d" % b, "RR%d" % b])
+            if c == 1:
+                for f in lv[1:2]:
+                    f()
+                if t == 1:
+                    dma("Y", "o0", T.yh[:, NI:NI + NV], T.H3[:, NI:NI + NV], ["H3l"], [])
+        for b in range(2):
+            a, e = BK[b]
+            vt(T.T0[:, SH + a:SH + e], pD[b][:, 0:e - a], T.RR[:, a:e], A.add, ["RR%d" % b, "T0t"], ["pD%d" % b, "T0%d" % b])
+            if b == 0:
+                vs(T.lst[:, 4:6, :], T.pW[:, 0:112], SH, A.add, [], ["pW", "l9", "l11"])
+        if t == 0:
+            vc(T.ZY[:], T.zero[:, 0:392], ["zero"], ["ZY"])
+            vc(T.ZX[:], T.zero[:, 0:520], ["zero"], ["ZX"])
+        tk = ["T00", "T01", "T0t"]
+        for c in range(4):
+            a, e = CQ[c]
+            op("S", lambda: S.activation(T.TT[:, a:e], T.T0[:].indirect(lst(KL, a, e)), F.Relu, bias=T.bias[:, 1:2]), tk + ["l1", "bias1"], ["TT%d" % c])
+            vt(T.KK[:, SH + a:SH + e], T.T0[:].indirect(lst(KR, a, e)), T.TT[:, a:e], A.max, tk + ["l3", "TT%d" % c], ["KK%d" % c])
+            if c < 2:
+                twin(T.K2[:, a:e], T.KK[:, SH + a:SH + e], e - a, "KK%d" % c, "K2%d" % c)
+        for c in (2, 3):
+            a, e = CQ[c]
+            sc(T.K2[:, a:e], T.KK[:, SH + a:SH + e], ["KK%d" % c], ["K2%d" % c])
+        kk, up, uu = four("KK") + ["KKp"], four("UP") + ["UPp"], four("UU") + ["UUp", "UUq"]
+        ny = 2 if last else 3
+        op("P", [const(T.pX, 0, -1, True), const(T.pX, 2, -1)] +
+           [mm(fld(T.pX, f), J2, ub((KL, KL, KR, KR)[f])) for f in range(4)] +
+           [mm(fld(T.pX, 4 + f), J1, ub((KR, KR, KL, KL)[f])) for f in range(4)], ["rows", "In1", "In2", "u1", "u3"], ["pX"])
+        op("P", [const(T.pY, 1, 1, True)] +
+           [mm(fld(T.pY, f), J1, ub((IDB, IDB, SB)[f])) for f in range(ny)] +
+           [mm(fld(T.pY, 4 + f), J1, ub((KL, KR, PA)[f])) for f in range(ny)] +
+           [mm(fld(T.pY, 4 + f), I1, ub(SB)) for f in range(ny)], ["u1", "u3", "u7", "u9", "u14"], ["pY"])
+        op("P", [mm(T.pS[0:UP, :, j, :], I1, ub((KL, KR, PA)[j]), j == 0) for j in range(ny)], ["u1", "u3", "u9"], ["pS"])
+        op("P", [m for j in range(ny) for m in tolist(j, T.ZS, j, False, j == 0)], ["z0", "z1", "z2"], ["pW"])
+        for c in range(4):
+            a, e = CQ[c]
+            vt(T.UPT[:, SH + a:SH + e], T.KK[:].indirect(lst(PA, a, e)), T.K2[:, a:e], A.is_lt, kk + ["K2%d" % c, "l9", "UPp"], ["UP%d" % c])
+            twin(T.U2[:, a:e], T.UPT[:, SH + a:SH + e], e - a, "UP%d" % c, "U2%d" % c)
+        sc(T.KP[:], T.KK[:].indirect(lst(PA)), kk + ["l9"], ["KP"])
+        op("P", wrap(T.KK, SH, T.sK[:], T.pX, 0, 8), kk + ["sK"], ["pX"])
+        for c in range(4):
+            a, e = CQ[c]
+            vt(T.UU[:, SH + a:SH + e], T.UPT[:].indirect(lst(SB, a, e)), T.U2[:, a:e], A.max, up + ["U2%d" % c, "l7", "UUp"], ["UU%d" % c])
+        sc(T.DD[:], T.UPT[:].indirect(lst(PA)), up + ["l9"], ["DD"])
+        op("P", wrap(T.KP, 0, T.sP[:, 0:8 * ny], T.pY, 0, ny), ["KP", "sP"], ["pY"])
+        op("P", wrap(T.UPT, SH, T.sGn[:], T.pX, 0, 4), up + ["sGn"], ["pX"])
+        vc(T.N1[:, 0:448], T.UU[:].indirect(lst(IC, 0, 448)), uu + ["l11"], ["N10"])
+        sc(T.N1[:, 448:NI], T.UU[:].indirect(lst(IC, 448, NI)), uu + ["l11"], ["N11"])
+        op("P", wrap(T.DD, 0, T.sGn[:, 0:8 * ny], T.pY, 0, ny), ["DD"], ["pY"])
+        op("P", wrap(T.UU, SH, T.sGp[:, 0:8 * ny], T.pY, 0, ny, True), uu + ["sGp"], ["pY"])
+        op("P", wrap(T.N1, 0, T.sGp[:], T.pX, 0, 4, True), ["N10", "N11"], ["pX"])
+        if t == 0:
+            ghosts(2)
+            last_fills()
+            send(2)
+        vs(T.EY[0:UP, 0:64 * ny], fld(T.pY, 0, ny), -4096.0, A.is_equal, [], ["pY", "EY"])
+        vt(zf(T.ZY, 0, ny), fld(T.pY, 4, ny), T.EY[0:UP, 0:64 * ny], A.mult, ["EY", "ZY"], ["pY", "ZY"])
+        op("P", [m for f in range(ny) for m in tolist(f, T.ZY, f)], ["ZY"], ["pW"])
+        op("P", [mm(T.pS[0:UP, :, f, :], I1, zf(T.ZY, f)) for f in range(ny)], ["ZY"], ["pS"])
+        vs(T.EQ[0:UP], fld(T.pX, 0, 4), -4096.0, A.is_equal, [], ["pX", "EQ"])
+        vt(zf(T.ZX, 0, 4), fld(T.pX, 4, 4), T.EQ[0:UP], A.mult, ["EQ", "ZX"], ["pX", "ZX"])
+
+        def lists():
+            op("P", [m for f in range(4) for m in tolist(1 - f // 2, T.ZX, f, f == 3)], ["ZX"], ["pW"])
+
+        def state():
+            op("P", [mm(T.pS[0:UP, :, 1 - f // 2, :], I1, zf(T.ZX, f), False, f == 3) for f in range(4)], ["ZX"], ["pS"])
+
+        def vlists():
+            vs(T.lst[:, 0:ny, :], T.pW[:, 0:56 * ny], SH, A.add, [], ["pW", "l1", "l3", "l5"])
+
+        def vstate():
+            vc(T.UB[0:UP, :, KL:2 * ny:2, :], T.pS[0:UP, :, 0:ny, :], ["UB"], ["pS", "u1", "u3", "u5"])
+
+        for f in ((lists, state, vlists, vstate) if last else (state, lists, vstate, vlists)):
+            f()
+        op("P", unwrap(pF[0], 0, True, True), uk, ["pF0"])
+        op("P", unwrap(pF[1], 1, True, True), uk, ["pF1"])
+
+        def newc(c):
+            a, e = CQ[c]
+            sc(T.BB[:, a:e], win.indirect(lst(KL, a, e)), hk + ["l1"], ["B%d" % c])
+
+        def newm(c):
+            a, e = CQ[c]
+            out = T.H3[:, a:e] if last else H[t + 1][:, SH + a:SH + e]
+            vt(out, win.indirect(lst(KR, a, e)), T.BB[:, a:e], A.max, hk + ["l3", "B%d" % c], ["H%d_%d" % (t + 1, c)])
+
+        if not last:
+            nt = ["NT0", "NT1", "NTp", "l5"]
+            op("P", [mm(fld(T.pX, f), J1, ub(ID), f == 0) for f in (0, 1)] + [mm(fld(T.pX, f), J1, ub(PP)) for f in (2, 3)] +
+               [mm(fld(T.pX, 4), I1, ub(PP)), const(T.pX, 5, 0)], ["u15", "u5"], ["pX"])
+            op("P", mm(T.pS[0:UP, :, 3, :], I1, ub(PP), True), ["u5"], ["pS"])
+            op("P", tolist(0, T.ZS, ZK[PA], False, True) + tolist(0, T.ZY, 2), ["z2", "ZY"], ["pW"])
+            newc(0)
+            vt(zf(T.ZS, ZK[IC]), ub(KL), ub(KR), A.min, ["u1", "u3", "ZS"], ["z3"])
+            vc(T.NT[:, SH:SH + 512], pF[0][:, 0:512], [], ["pF0", "NT0"])
+            sc(T.NT[:, SH + 512:SH + NI], pF[1][:, 0:384], [], ["pF1", "NT1"])
+            vc(T.NP[:, 0:448], T.NT[:].indirect(lst(PP, 0, 448)), nt, ["NP0"])
+            sc(T.NP[:, 448:NI], T.NT[:].indirect(lst(PP, 448, NI)), nt, ["NP1"])
+            op("P", wrap(T.NP, 0, T.sN[:], T.pX, 0, 6, True), ["NP0", "NP1", "sN"], ["pX"])
+            for c in range(1, 4):
+                newc(c)
+            newm(0)
+            for j in range(2):
+                vc(zf(T.ZS, j), ub((KL, KR)[j]), ["u1", "u3", "ZS"], ["z%d" % j])
+            newm(1)
+            newm(2)
+            vs(T.EQ[0:UP, 0:128], fld(T.pX, 0, 2), 0.0, A.is_equal, [], ["pX", "EQ"])
+            vt(zf(T.ZX, 0, 2), fld(T.pX, 2, 2), T.EQ[0:UP, 0:128], A.mult, ["EQ", "ZX"], ["pX", "ZX"])
+            op("P", tolist(0, T.ZX, 0) + tolist(0, T.ZX, 1, True), ["ZX"], ["pW"])
+            op("P", [mm(T.pS[0:UP, :, 3, :], I1, zf(T.ZX, f), False, f == 1) for f in range(2)], ["ZX"], ["pS"])
+            vt(T.EY[0:UP, 0:64], T.EQ[0:UP, 0:64], T.EQ[0:UP, 64:128], A.add, ["EQ"], ["EY"])
+            newm(3)
+            vs(lst(SB), T.pW[:, 0:56], SH, A.add, [], ["pW", "l7"])
+            vt(T.EY[0:UP, 64:128], fld(T.pX, 4), T.EY[0:UP, 0:64], A.mult, ["EY"], ["pX", "EY1"])
+            vc(ub(SB), T.pS[0:UP, :, 3, :], ["UB"], ["pS", "u7"])
+            vt(ub(PA), fld(T.pX, 5), T.EY[0:UP, 64:128], A.add, ["EY1", "UB"], ["pX", "u9"])
+            vc(zf(T.ZS, ZK[PA]), ub(PA), ["u9", "ZS"], ["z2"])
+        else:
+            for c in range(4):
+                a, e = CQ[c]
+                newc(c)
+                newm(c)
+                if c > 0:
+                    a = 0 if c == 1 else a
+                    dma("Y", "o%d" % c, T.yh[:, a:e], T.H3[:, a:e], ["H3_0", "H3_%d" % c], [])
+            sc(T.NT[:, SH:SH + 512], pF[0][:, 0:512], [], ["pF0", "NT0"])
+            sc(T.NT[:, SH + 512:SH + NI], pF[1][:, 0:384], [], ["pF1", "NT1"])
+            dma("S", "o4", T.yk[:, 0:NI], T.NT[KL::16, SH:SH + NI], ["NT0", "NT1"], [])
+            dma("Y", "o5", T.yk[:, NI:2 * NI], T.NT[KR::16, SH:SH + NI], ["NT0", "NT1"], [])
+
+    for s in top:
+        need("G", (s, top[s]))

@@ -8,29 +8,34 @@ TW = 1808
 GH = NI + NV + SH
 NO = 2 * NI + 1
 UP = 112
-KL, KR, PP, SB, PA, IDB, ID = 1, 3, 5, 7, 9, 14, 15
-IC = 11
-CH = [(0, 192), (192, 512), (512, 704), (704, 896)]
-CQ = [(0, 224), (224, 448), (448, 672), (672, 896)]
-BK = [(0, 512), (512, 896)]
+HB = NI // 2
+KL, KR, SB, PA, ID, IDB, MC, MD = 1, 2, 3, 4, 5, 6, 7, 8
+IC = 5
+RND = 12582912.0
+CG = [(0, 128), (128, 448), (448, 768), (768, 896)]
+CK = [(0, 96), (96, 288), (288, 480), (480, 704), (704, 896)]
+CU = [(0, 288), (288, 480), (480, 704), (704, 896)]
+CO = [(0, 96), (96, 320), (320, 544), (544, 768), (768, 896)]
+N1A, N1V, NPS = 224, 448, 672
+BX, BY, D0, D1, F0, F1, BW, BS = range(8)
 F32, F16, B16 = "float32", "float16", "bfloat16"
 
-SCRATCH = {"kks": ("sbuf", [128, 2, 56], "int32"), "lst": ("sbuf", [128, 6, 56], "uint16"), "slu": ("sbuf", [128, 28], "uint16"),
-           "UB": ("sbuf", [128, 8, 16, 8], F16), "ZX": ("sbuf", [128, 65, 8], F16), "ZY": ("sbuf", [128, 49, 8], F16),
-           "ZS": ("sbuf", [128, 65, 8], F16), "WP": ("sbuf", [128, 2, 2, UP], F16), "Ih3": ("sbuf", [128, 8, 16], F16),
-           "sW": ("sbuf", [128, 2, 16], F32), "crow": ("sbuf", [128, 8, 16], B16), "pS": ("psum", [128, 8, 8, 8], F32)}
-for _dt, _bufs in (("int32", dict(h0s=1352, vels=452, sls=28, pi=128)),
+SCRATCH = {"kks": ("sbuf", [128, 2, 56], "int32"), "lst": ("sbuf", [128, 5, 56], "uint16"), "slu": ("sbuf", [128, 28], "uint16"),
+           "UB": ("sbuf", [128, 8, 16, 8], F16), "UK": ("sbuf", [128, 144, 8], F16), "ZX": ("sbuf", [128, 81, 8], F16),
+           "ZY": ("sbuf", [128, 65, 8], F16), "ZP": ("sbuf", [128, 65, 8], F16), "ZS": ("sbuf", [128, 81, 8], F16),
+           "WP": ("sbuf", [128, 2, 2, UP], F16), "Ih3": ("sbuf", [128, 8, 16], F16), "MK": ("sbuf", [128, 3, 128], F32),
+           "sW": ("sbuf", [128, 2, 16], F32), "crow": ("sbuf", [128, 8, 16], B16),
+           "PS": ("psum", [128, 7 * 512], F32), "pS": ("psum", [128, 8, 8, 8], F32)}
+for _dt, _bufs in (("int32", dict(h0s=1352, vels=452, sls=28)),
                    (B16, dict(velb=456, H0=TW, H1=TW, H2=TW, sb0=448, sb1=448, sb2=448, AA=NI, BB=NI, M0=NI, M1=NI, UPT=TW, UU=TW,
-                              U2=NI, DD=NI, N1=NI, one=512, Ib=128, Bp=128, Bn=128, sGp=32, sGn=32, zero=528, rows=256)),
-                   (F32, dict(LZ=452, H3=1348, vals=NI, W1=TW, W2=TW, RR=NI, T0=TW, TT=NI, KK=912, K2=NI, KP=NI, NT=912, NP=NI,
-                              EQ=256, EY=192, onef=64, cw=16, sK=64, sP=24, sN=48, iv=64, bt=24, bias=2)),
-                   (F16, dict(Ih=128, In1=128, In2=128))):
+                              U2=NI, DD=NI, N1=NI, one=HB, Ib=128, Bp=128, Bn=128, sGp=48, sGn=48, sN=64, zero=648, rows=64)),
+                   (F32, dict(LZ=452, H3=1348, vals=NI, W1=TW, W2=TW, RR=NI, T0=TW, TT=NI, KK=912, K2=NI, KP=NI, NT=912, NK=224,
+                              EQ=256, onef=16, cw=16, nb=64, nb2=16, sK=64, sP=64, iv=64, iv2=128, bt=32, bias=4)),
+                   (F16, dict(Ih=128, In1=128, In2=128, idc=128, NP=NI))):
     for _k in _bufs:
         SCRATCH[_k] = ("sbuf", [128, _bufs[_k]], _dt)
-for _k in ("pD0", "pD1", "pF0", "pF1", "pX", "pY", "pW"):
-    SCRATCH[_k] = ("psum", [128, 512], F32)
 SEMAPHORES = ["cV", "cS", "cP", "cG", "dsl", "dlf", "dkl", "dkr", "dhi", "dve", "arr0", "arr1", "arr2", "sent",
-              "o0", "o1", "o2", "o3", "o4", "o5"]
+              "f0", "f1", "f2", "f3", "o0", "o1", "o2", "o3", "o4", "o5"]
 
 
 def rank_program(g, core, T, topo):
@@ -79,16 +84,14 @@ def rank_program(g, core, T, topo):
         ins.then_inc(T.sem["c" + e], 1)
         note(("c" + e, cnt[e]), r, w)
 
-    def dma(e, sem, out, in_, r, w):
+    def dma(e, sem, pairs, r, w):
         order(e, r, w)
-        Q[e].dma_start(out, in_).then_inc(T.sem[sem], 16)
-        note((sem, top.get(sem, 0) + 16), r, w)
+        for out, in_ in pairs:
+            Q[e].dma_start(out, in_).then_inc(T.sem[sem], 16)
+        note((sem, top.get(sem, 0) + 16 * len(pairs)), r, w)
 
     V, S, P = g.vector, g.scalar, g.tensor
     H = [T.H0, T.H1, T.H2, T.H3]
-    pD, pF = [T.pD0, T.pD1], [T.pF0, T.pF1]
-    LK = {KL: 0, KR: 1, PP: 2, SB: 3, PA: 4, IC: 5}
-    ZK = {KL: 0, KR: 1, PA: 2, IC: 3}
     I1, J1, J2 = T.Ih[0:UP, 0:UP], T.In1[0:UP, 0:UP], T.In2[0:UP, 0:UP]
 
     def vc(out, in_, r, w):
@@ -103,54 +106,66 @@ def rank_program(g, core, T, topo):
     def sc(out, in_, r, w):
         op("S", lambda: S.activation(out, in_, F.Copy), r, w)
 
-    def four(k):
-        return ["%s%d" % (k, c) for c in range(4)]
+    def names(k, n=4):
+        return ["%s%d" % (k, c) for c in range(n)]
+
+    def pb(*banks):
+        return ["p%d" % b for b in banks]
+
+    def bank(b, a, e, parts=128):
+        return T.PS[0:parts, 512 * b + a:512 * b + e]
+
+    def fld(b, f, n=1):
+        return bank(b, 64 * f, 64 * (f + n), UP)
 
     def lst(t, a=0, b=NI):
-        return T.lst[:, LK[t], a // 16:b // 16]
+        return T.lst[:, t - 1, a // 16:b // 16]
 
     def ub(t):
         return T.UB[0:UP, :, t, :]
-
-    def fld(ps, f, n=1):
-        return ps[0:UP, 64 * f:64 * (f + n)]
 
     def zf(Z, f, n=1):
         return Z[0:UP, 16 * f + 1:16 * (f + n):2, :]
 
     def hkeys(t):
-        return four("H%d_" % t) + ["H%dl" % t, "H%dg" % t, "H%dp" % t]
+        return names("H%d_" % t, 5) + ["H%dl" % t, "H%dg" % t, "H%dp" % t]
 
     def mm(out, lhsT, rhs, start=False, stop=False):
         return lambda: P.matmul(out, lhsT, rhs, start, stop)
 
-    def const(ps, f, v, start=False):
-        a = {-1: 0, 0: 64, 1: 192}[v]
-        return mm(fld(ps, f), T.one[0:1, 0:UP], T.rows[0:1, a:a + 64], start)
+    def less1(out, start=False):
+        return mm(out, T.one[0:1, 0:UP], T.rows[0:1, :], start)
 
-    def wrap(tab, off, rhs, ps, f0, nf, stop=False, start=False):
-        return [mm(ps[0:UP, 64 * f0 + r:64 * (f0 + nf):8], tab[:, off + r:off + NI:8], rhs, start and r == 0, stop and r == 7)
+    def wrap(tab, off, rhs, b, nf, stop=False, start=False):
+        return [mm(T.PS[0:UP, 512 * b + r:512 * b + 64 * nf:8], tab[:, off + r:off + NI:8], rhs, start and r == 0, stop and r == 7)
                 for r in range(8)]
 
-    def unwrap(ps, b, start=False, stop=False):
-        a, e = BK[b]
-        return [mm(ps[:, r:e - a:8], T.UB[0:UP, :, :, r], T.Ih[0:UP, a // 8:e // 8], start, stop) for r in range(8)]
+    def unwrap(h, alone):
+        b = D0 + h
+        return [mm(T.PS[:, 512 * b + r:512 * b + HB:8], T.UB[0:UP, :, :, r], T.Ih[0:UP, 56 * h:56 * h + 56], alone, alone) for r in range(8)]
 
-    def tolist(j, Z, f, stop=False, start=False):
-        return [mm(T.pW[:, 56 * j:56 * j + 56], Z[0:UP, 16 * f + 1 - h:16 * f + 17 - h, :], T.Ih[0:UP, h:UP:2],
+    def tolist(b, j, Z, f, start=False, stop=False, eye=T.Ih):
+        return [mm(bank(b, 56 * j, 56 * j + 56), Z[0:UP, 16 * f + 1 - h:16 * f + 17 - h, :], eye[0:UP, h:UP:2],
                    start and h == 0, stop and h == 1) for h in range(2)]
+
+    def cast(t, n, b):
+        op("S", lambda: S.activation(T.lst[:, t - 1:t - 1 + n, :], bank(b, 0, 56 * n), F.Identity, bias=float(SH)), [],
+           pb(b) + ["l%d" % (t + j) for j in range(n)])
+
+    def st(j):
+        return T.pS[0:UP, :, j, :]
 
     def fill(out, n, val, r, w):
         op("G", lambda: g.iota(out, [[0, n]], val, 0, allow_small_or_imprecise_dtypes=True), r, w)
 
-    def pick(out, src, pat, t, keys):
-        op("G", lambda: g.affine_select(out, src, pat, A.is_equal, 0.0, -t, 1), ["one", "onef", "cw"], keys)
+    def pick(out, src, pat, t, r, w):
+        op("G", lambda: g.affine_select(out, src, pat, A.is_equal, 0.0, -t, 1), r, w)
 
-    def put(out, src, pat, t, val, keys):
-        op("G", lambda: g.affine_select(out, src, pat, A.not_equal, val, -t, 1), keys + ["zero"], keys)
+    def put(out, src, pat, t, val, r, w):
+        op("G", lambda: g.affine_select(out, src, pat, A.not_equal, val, -t, 1), r, w)
 
     def twin(out, src, n, r, w):
-        op("G", lambda: g.affine_select(out, src, [[0, n]], A.is_ge, 0.0, 0, 0), [r], [w])
+        op("G", lambda: g.affine_select(out, src, [[0, n]], A.is_ge, 0.0, 0, 0), r, w)
 
     def send(t):
         trs = []
@@ -164,302 +179,343 @@ def rank_program(g, core, T, topo):
         g.remote_dma_fused(trs, local_sem=T.sem.sent)
         top["sent"] = top.get("sent", 0) + N - 1
 
-    def leaves(t, ps, key):
-        op("P", [mm(ps[:, 0:NV], T.Ib[:], H[t][:, NI + SH:GH], True, False), mm(ps[:, 0:NV], T.Ib[:], T.velb[:, 0:NV], False, True)],
-           ["Ib", "H%dl" % t, "velb"], [key])
+    def leaves(t, b):
+        ps = bank(b, 0, NV)
+        op("P", [mm(ps, T.Ib[:], H[t][:, NI + SH:GH], True, False), mm(ps, T.Ib[:], T.velb[:, 0:NV], False, True)],
+           ["Ib", "H%dl" % t, "velb"], pb(b))
         out = T.H3[:, NI:NI + NV] if t == RO - 1 else H[t + 1][:, NI + SH:GH]
-        return [lambda: op("S", lambda: S.activation(T.LZ[:, 0:NV], ps[:, 0:NV], F.Relu, bias=255.0, scale=-1.0), [], [key, "LZ"]),
+        return [lambda: op("S", lambda: S.activation(T.LZ[:, 0:NV], ps, F.Relu, bias=255.0, scale=-1.0), [], pb(b) + ["LZ"]),
                 lambda: op("S", lambda: S.activation(out, T.LZ[:, 0:NV], F.Relu, bias=255.0, scale=-1.0), ["LZ"], ["H%dl" % (t + 1)])]
 
     def ghosts(t):
-        sc(T["sb%d" % t][:], H[t][:, NI:GH].indirect(T.slu[:]), ["slu", "H%dl" % t, "H%d_3" % t], ["sb%d" % t])
+        sc(T["sb%d" % t][:], H[t][:, NI:GH].indirect(T.slu[:]), ["slu", "H%dl" % t, "H%dq" % t], ["sb%d" % t])
 
     for t in range(RO):
         wr["H%dg" % t] = ("arr%d" % t, N - 1)
         top["arr%d" % t] = N - 1
 
-    dma("Y", "dkl", T.kks[:, 0, :], T.kl[:], [], ["kk0"])
-    dma("S", "dkr", T.kks[:, 1, :], T.kr[:], [], ["kk1"])
-    dma("Y", "dlf", T.h0s[:, NI:GH], T.h0[:, NI - SH:NI + NV], [], ["h0l"])
-    dma("S", "dsl", T.sls[:], T.sl[:], [], ["sls"])
-    dma("Y", "dve", T.vels[:, 0:NV], T.vel[:], [], ["vels"])
-    dma("Y", "dhi", T.h0s[:, SH:NI], T.h0[:, 0:NI - SH], [], ["h0i"])
+    dma("Y", "dkl", [(T.kks[:, 0, :], T.kl[:])], [], ["kk0"])
+    dma("S", "dkr", [(T.kks[:, 1, :], T.kr[:])], [], ["kk1"])
+    dma("Y", "dlf", [(T.h0s[:, NI:GH], T.h0[:, NI - SH:NI + NV])], [], ["h0l"])
+    dma("S", "dsl", [(T.sls[:], T.sl[:])], [], ["sls"])
+    dma("Y", "dve", [(T.vels[:, 0:NV], T.vel[:])], [], ["vels"])
+    dma("Y", "dhi", [(T.h0s[:, SH:NI], T.h0[:, 0:NI - SH])], [], ["h0i"])
 
+    G8 = [[-16, 8]]
+    op("V", lambda: V.memset(T.one[:, 0:128], 1.0), [], ["one"])
     op("V", lambda: V.memset(T.zero[:], 0.0), [], ["zero"])
-    op("V", lambda: V.memset(T.one[:], 1.0), [], ["one"])
     op("G", lambda: g.iota(T.iv[:], [[0, 8], [1, 8]], 0, 8, allow_small_or_imprecise_dtypes=True), [], ["iv"])
     op("G", lambda: g.affine_select(T.Ib[:], T.one[:, 0:128], [[-1, 128]], A.is_equal, 0.0, 0, 1), ["one"], ["Ib"])
-    fill(T.W2[:, 0:904], 904, 0, [], ["W2"])
-    op("S", lambda: S.activation(T.W1[:, 0:512], T.zero[:, 0:512], F.Silu), ["zero"], ["W1"])
-    op("S", lambda: S.activation(T.W1[:, 512:904], T.zero[:, 0:392], F.Silu), ["zero"], ["W1"])
+    op("S", lambda: S.activation(T.W1[:, 0:64], T.one[:, 0:64], F.Silu, scale=0.0), ["one"], ["W1"])
+    sc(T.W1[:, 64:512], T.zero[:, 0:448], ["zero"], ["W1"])
+    sc(T.W1[:, 512:904], T.zero[:, 0:392], ["zero"], ["W1"])
+    op("V", lambda: V.memset(T.onef[:], 1.0), [], ["onef"])
+    op("V", lambda: V.memset(T.cw[:], -1.0 / 32), [], ["cw"])
     vc(T.WP[:], T.zero[:, 0:448], ["zero"], ["WP"])
     for j in range(2):
         vc(T.UB[:, 4 * j:4 * j + 4], T.zero[:, 0:512], ["zero"], ["UB"])
-    vc(T.Ih[:], T.Ib[:], ["Ib"], ["Ih"])
+    pick(T.bt[:, 0:8], T.onef[:, 0:8], G8, ID, ["onef"], ["bt0"])
+    fill(T.W2[:, 0:904], 904, 0, [], ["W2"])
     vc(T.Ih3[:], T.Ib[:], ["Ib"], ["Ih3"])
-    vc(ub(ID), T.iv[0:UP], ["iv", "UB"], ["u15"])
-    vc(T.ZS[:], T.zero[:, 0:520], ["zero"], ["ZS"])
-    op("V", lambda: V.memset(T.onef[:], 1.0), [], ["onef"])
-    op("V", lambda: V.memset(T.cw[:], -1.0 / 32), [], ["cw"])
+    vc(T.Ih[:], T.Ib[:], ["Ib"], ["Ih"])
+    vc(ub(ID), T.iv[0:UP], ["iv", "UB"], ["u5"])
+    pick(T.sW[:, 0, 0:8], T.cw[:, 0:8], G8, KR, ["cw"], ["sW0"])
+    pick(T.sW[:, 0, 8:16], T.cw[:, 0:8], G8, ID, ["cw"], ["sW0"])
+    pick(T.sW[:, 1, 0:8], T.cw[:, 0:8], G8, KL, ["cw"], ["sW1"])
+    pick(T.sW[:, 1, 8:16], T.cw[:, 0:8], G8, ID, ["cw"], ["sW1"])
+    dma("Y", "f0", [(T[k][:, a:a + 448], T.zero[:, 0:448]) for k in ("UPT", "UU") for a in (912, 1360)], ["zero", "h0l"], ["UPr"])
+    sc(T.ZX[:], T.zero[:], ["zero"], ["ZX"])
+    dma("Y", "f1", [(T.ZS[:], T.ZX[:])], ["ZX"], ["ZS"])
+    dma("Y", "f2", [(T.ZY[:], T.ZX[:, 0:65]), (T.ZP[:], T.ZX[:, 0:65]), (T.UK[:, 0:72], T.ZX[:, 0:72]), (T.UK[:, 72:144], T.ZX[:, 0:72])],
+        ["ZX"], ["ZY", "ZP", "UK"])
 
     for h in range(2):
         vc(T.WP[:, :, h, h:UP:2], T.kks[:], ["kk0", "kk1", "WP"], ["WP%d" % h])
-    op("P", [mm(T.pS[0:UP, :, j, :], T.WP[:, j, h, :], T.Ih3[:, :, 8 * h:8 * h + 8], j + h == 0, j + h == 2) for j in range(2) for h in range(2)],
-       ["WP0", "WP1", "Ih3"], ["pS"])
+    op("P", [mm(st(j), T.WP[:, j, h, :], T.Ih3[:, :, 8 * h:8 * h + 8], j + h == 0, j + h == 2) for j in range(2) for h in range(2)],
+       ["WP0", "WP1", "Ih3"], pb(BS))
     vs(T.slu[:], T.sls[:], SH, A.add, ["sls"], ["slu"])
-    vs(T.lst[:, 0:2, :], T.kks[:], SH, A.add, ["kk0", "kk1"], ["l1", "l3"])
-    vc(T.UB[0:UP, :, KL:KR + 1:2, :], T.pS[0:UP, :, 0:2, :], ["UB"], ["pS", "u1", "u3"])
-    op("P", unwrap(pF[0], 0, True, True), ["UB", "u1", "u3", "u15", "Ih"], ["pF0"])
-    op("P", unwrap(pF[1], 1, True, True), ["UB", "u1", "u3", "u15", "Ih"], ["pF1"])
-    vc(T.sb0[:], T.h0s[:, NI:GH].indirect(T.slu[:]), ["slu", "h0l"], ["sb0"])
+    op("V", lambda: V.tensor_reduce(T.bt[:, 24:25], T.bt[:, 0:8], AxisListType.X, A.add), ["bt0"], ["bt3"])
+    vc(T.UB[0:UP, :, KL:KR + 1, :], T.pS[0:UP, :, 0:2, :], ["UB"], pb(BS) + ["u1", "u2"])
+    for h in range(2):
+        op("P", unwrap(h, True), ["UB", "u1", "u2", "u5", "Ih"], pb(D0 + h))
+    op("V", lambda: V.tensor_scalar(T.bias[:, 2:3], T.bt[:, 24:25], 32.0 * (NI - NO), 32.0 * NO, A.mult, A.add), ["bt3"], ["bias2"])
+    vs(T.lst[:, 0:2, :], T.kks[:], SH, A.add, ["kk0", "kk1"], ["l1", "l2"])
+    sc(T.sb0[:], T.h0s[:, NI:GH].indirect(T.slu[:]), ["slu", "h0l"], ["sb0"])
     send(0)
-    for b in range(2):
-        a, e = BK[b]
-        op("S", lambda: S.activation(T.vals[:, a:e], pF[b][:, 0:e - a], F.Identity, bias=32.0 * NO, scale=-32.0), [], ["pF%d" % b, "vals%d" % b])
-    op("S", lambda: S.activation(T.W2[:].indirect(lst(KR)), T.vals[:], F.Silu), ["vals0", "vals1", "l3", "W2"], ["W2"])
-    vc(T.H0[:, NI + SH:GH], T.h0s[:, NI + SH:GH], ["h0l"], ["H0l"])
-    vc(T.velb[:, 0:NV], T.vels[:, 0:NV], ["vels"], ["velb"])
-    for f in leaves(0, T.pY, "pY"):
-        f()
-    vc(T.W1[:].indirect(lst(KL)), T.vals[:], ["vals0", "vals1", "l1", "W1"], ["W1"])
+    op("V", lambda: V.tensor_scalar(T.vals[:, 0:HB], bank(D0, 0, HB), -32.0, T.bias[:, 2:3], A.mult, A.add), ["bias2"], pb(D0) + ["vals0"])
+    op("S", lambda: S.activation(T.vals[:, HB:NI], bank(D1, 0, HB), F.Identity, bias=T.bias[:, 2:3], scale=-32.0), ["bias2"], pb(D1) + ["vals1"])
+    vc(T.W1[:].indirect(lst(KL, 0, HB)), T.vals[:, 0:HB], ["vals0", "l1", "W1"], ["W1"])
+    vc(T.W1[:].indirect(lst(KL, HB, NI)), T.vals[:, HB:NI], ["vals1", "l1", "W1"], ["W1"])
+    op("S", lambda: S.activation(T.W2[:].indirect(lst(KR)), T.vals[:], F.Silu), ["vals0", "vals1", "l2", "W2"], ["W2"])
 
-    G8 = [[-16, 8]]
-    pick(T.sW[:, 0, 0:8], T.cw[:, 0:8], G8, KR, ["sW0"])
-    pick(T.sW[:, 0, 8:16], T.cw[:, 0:8], G8, ID, ["sW0"])
-    pick(T.sW[:, 1, 0:8], T.cw[:, 0:8], G8, KL, ["sW1"])
-    pick(T.sW[:, 1, 8:16], T.cw[:, 0:8], G8, ID, ["sW1"])
-    fill(T.H1[:, NI:NI + SH], SH, 0, [], ["H1_3"])
-    fill(T.Bp[:], 128, 4096, [], ["Bp"])
-    op("G", lambda: g.affine_select(T.Bp[:], T.Bp[:], [[-16, 8], [0, 16]], A.is_ge, 0.0, 0, 1), ["Bp"], ["Bp"])
-    op("G", lambda: g.affine_select(T.Bp[:], T.Bp[:], [[16, 8], [0, 16]], A.is_ge, 0.0, 15, -1), ["Bp"], ["Bp"])
+    fill(T.H1[:, NI:NI + SH], SH, 0, [], ["H1q"])
     fill(T.H0[:, 0:SH], SH, 0, [], ["H0p"])
     fill(T.H0[:, TW - 8:TW], 8, 0, [], ["H0p"])
+    fill(T.Bp[:], 128, 4096, [], ["Bp"])
     fill(T.crow[:], 128, -4096, [], ["crow"])
+    op("G", lambda: g.affine_select(T.Bp[:], T.Bp[:], [[-16, 8], [0, 16]], A.is_ge, 0.0, 0, 1), ["Bp"], ["Bp"])
     fill(T.crow[:, :, PA], 8, -2048, ["crow"], ["crow"])
-    pick(T.bt[:, 0:8], T.onef[:, 0:8], G8, IDB, ["bt"])
-    pick(T.bt[:, 8:16], T.onef[:, 0:8], G8, PA, ["bt"])
+    op("G", lambda: g.affine_select(T.Bp[:], T.Bp[:], [[16, 8], [0, 16]], A.is_ge, 0.0, 15, -1), ["Bp"], ["Bp"])
+    pick(T.bt[:, 8:16], T.onef[:, 0:8], G8, IDB, ["onef"], ["bt1"])
+    pick(T.bt[:, 16:24], T.onef[:, 0:8], G8, PA, ["onef"], ["bt2"])
+    fill(T.T0[:, 904:1356], 452, -4096, [], ["T0u"])
+    dma("Y", "f3", [(T.T0[:, 1356:TW], T.T0[:, 904:1356])], ["T0u"], ["T0v"])
 
-    op("P", wrap(T.W2, SH, T.sW[:, 1, :], T.pX, 0, 2, False, True), ["W2", "sW1"], ["pX"])
-    op("P", wrap(T.W1, SH, T.sW[:, 0, :], T.pX, 0, 2, True), ["W1", "sW0"], ["pX"])
-    vc(T.H0[:, SH:SH + NI], T.h0s[:, SH:SH + NI], ["h0i", "h0l"], four("H0_"))
-    vs(T.Bn[:], T.Bp[:], -1.0, A.mult, ["Bp"], ["Bn"])
-    op("V", lambda: V.tensor_scalar(ub(IDB), T.iv[0:UP], 2.0, 1.0, A.mult, A.add), ["iv", "UB"], ["u14"])
-    vs(T.pi[0:UP, 0:64], fld(T.pX, 0), float(NO), A.add, [], ["pX", "pi0"])
-    op("V", lambda: V.tensor_scalar(T.pi[0:UP, 64:128], fld(T.pX, 1), float(NO), float(NI), A.add, A.min), [], ["pX", "pi1"])
-    vc(zf(T.ZS, ZK[KL]), T.pi[0:UP, 0:64], ["pi0", "ZS"], ["z0"])
-    op("P", tolist(0, T.ZS, ZK[KL], True, True), ["z0", "ZS"], ["pW"])
-    vc(ub(SB), T.pi[0:UP, 0:64], ["pi0", "UB"], ["u7"])
-    vc(ub(PA), T.pi[0:UP, 64:128], ["pi1", "UB"], ["u9"])
-    vc(zf(T.ZS, ZK[PA]), T.pi[0:UP, 64:128], ["pi1", "ZS"], ["z2"])
-    vs(lst(SB), T.pW[:, 0:56], SH, A.add, [], ["pW", "l7"])
-    vt(zf(T.ZS, ZK[IC]), ub(KL), ub(KR), A.min, ["u1", "u3", "ZS"], ["z3"])
-    op("V", lambda: V.tensor_reduce(T.bias[:, 0:1], T.bt[:, 0:8], AxisListType.X, A.add, negate=True), ["bt"], ["bias0"])
-    op("V", lambda: V.tensor_reduce(T.bt[:, 16:17], T.bt[:, 8:16], AxisListType.X, A.add), ["bt"], ["bt8"])
-
-    def late():
-        for j in range(2):
-            vc(zf(T.ZS, j), ub((KL, KR)[j]), ["u1", "u3", "ZS"], ["z%d" % j])
-        vs(T.In1[:], T.Ib[:], -1.0, A.mult, ["Ib"], ["In1"])
-        vs(T.In2[:], T.Ib[:], -2.0, A.mult, ["Ib"], ["In2"])
-        op("V", lambda: V.tensor_scalar(T.bias[:, 1:2], T.bt[:, 16:17], -2048.0, 2048.0, A.mult, A.add), ["bt8"], ["bias1"])
-
+    op("P", wrap(T.W1, SH, T.sW[:, 0, :], BX, 2, False, True), ["W1", "sW0"], pb(BX))
+    op("P", wrap(T.W2, SH, T.sW[:, 1, :], BX, 2, True), ["W2", "sW1"], pb(BX))
+    vt(T.LZ[:, 0:NV], T.h0s[:, NI + SH:GH], T.vels[:, 0:NV], A.add, ["h0l", "vels"], ["LZ"])
+    sc(T.H0[:, SH:SH + NI], T.h0s[:, SH:SH + NI], ["h0i", "h0l"], names("H0_", 5))
+    vc(T.H0[:, NI + SH:GH], T.h0s[:, NI + SH:GH], ["h0l"], ["H0l"])
+    op("V", lambda: V.tensor_scalar(T.H1[:, NI + SH:GH], T.LZ[:, 0:NV], 0.0, 255.0, A.max, A.min), ["LZ"], ["H1l"])
+    sc(T.velb[:, 0:NV], T.vels[:, 0:NV], ["vels"], ["velb"])
     ghosts(1)
-    for j in range(2):
-        sc(T.UU[:, NI + 456 * j:NI + 456 * j + 456], T.zero[:, 0:456], ["zero"], ["UUp"])
-    fill(T.T0[:, NI:TW], TW - NI, -4096, [], ["T0t"])
-    fill(T.T0[:, 0:SH], SH, 0, [], ["T0t"])
+    op("V", lambda: V.memset(T.one[:, 128:HB], 1.0), [], ["one1"])
+
+    def whole(out, f, base, r, w):
+        op("V", lambda: V.tensor_scalar(out, fld(BX, f), RND + base, -RND, A.add, A.add), r, pb(BX) + w)
+
+    whole(zf(T.ZS, SB - 1), 0, NO, ["ZS"], ["z3"])
+    op("P", tolist(BW, 0, T.ZS, SB - 1, True, True), ["z3", "ZS"], pb(BW))
+    whole(zf(T.ZS, PA - 1), 1, NI, ["ZS"], ["z4"])
+    cast(SB, 1, BW)
+    vs(T.Bn[:], T.Bp[:], -1.0, A.mult, ["Bp"], ["Bn"])
+    op("V", lambda: V.tensor_scalar(ub(IDB), T.iv[0:UP], 2.0, 1.0, A.mult, A.add), ["iv", "UB"], ["u6"])
+    vc(ub(SB), zf(T.ZS, SB - 1), ["z3", "UB"], ["u3"])
+    vc(ub(PA), zf(T.ZS, PA - 1), ["z4", "UB"], ["u4"])
+    vt(zf(T.ZS, IC - 1), ub(KL), ub(KR), A.min, ["u1", "u2", "ZS"], ["z5"])
+    op("V", lambda: V.tensor_reduce(T.bias[:, 0:1], T.bt[:, 8:16], AxisListType.X, A.add, negate=True), ["bt1"], ["bias0"])
+    op("V", lambda: V.tensor_reduce(T.bt[:, 25:26], T.bt[:, 16:24], AxisListType.X, A.add), ["bt2"], ["bt4"])
+
+    def zcopy(t):
+        twin(zf(T.ZS, t - 1), ub(t), 64, ["u%d" % t, "ZS"], ["z%d" % t])
+
     send(1)
-    op("G", lambda: g.iota(T.rows[:], [[1, 2], [1, 2], [0, 64]], -1, 0, allow_small_or_imprecise_dtypes=True), [], ["rows"])
-    fill(T.H2[:, NI:NI + SH], SH, 0, [], ["H2_3"])
+    fill(T.T0[:, 0:SH], SH, 0, [], ["T0t"])
+    fill(T.T0[:, NI:904], 8, -4096, [], ["T0t"])
     fill(T.KK[:, 0:SH], SH, 0, [], ["KKp"])
     fill(T.KK[:, SH + NI:912], 912 - SH - NI, 0, [], ["KKp"])
-    fill(T.UPT[:, NI:TW], TW - NI, 0, [], ["UPp"])
-    fill(T.UPT[:, 0:SH], SH, 0, [], ["UPp"])
-    pick(T.sK[:, 0:32], T.onef[:, 0:32], [[0, 4]] + G8, IDB, ["sK"])
-    pick(T.sK[:, 32:64], T.onef[:, 0:32], [[0, 2], [-2, 2]] + G8, KL, ["sK"])
-    put(T.sK[:], T.sK[:], [[0, 8]] + G8, 0, -1.0, ["sK"])
-    put(T.sGp[:], T.zero[:, 0:32], [[0, 4]] + G8, PA, 4096.0, ["sGp"])
-    put(T.sGn[:], T.zero[:, 0:32], [[0, 4]] + G8, PA, -4096.0, ["sGn"])
-    pick(T.sP[:, 0:16], T.onef[:, 0:16], [[0, 2]] + G8, IDB, ["sP"])
-    pick(T.sP[:, 16:24], T.onef[:, 0:8], G8, ID, ["sP"])
-    put(T.sP[:], T.sP[:], [[0, 3]] + G8, 0, -1.0, ["sP"])
-    fill(T.UU[:, 0:SH], SH, 0, [], ["UUq"])
+    fill(T.rows[:], 64, -1, [], ["rows"])
+    put(T.nb[:], T.zero[:, 0:64], [[0, 8]] + G8, 0, -1.0, ["zero"], ["nb"])
+    op("G", lambda: g.iota(T.iv2[:], [[0, 8], [-1, 2], [2, 8]], 1, 16, allow_small_or_imprecise_dtypes=True), [], ["iv2"])
+    put(T.sK[:, 0:32], T.nb[:, 0:32], [[0, 4]] + G8, IDB, 1.0, ["nb"], ["sK"])
+    put(T.sK[:, 32:64], T.nb[:, 0:32], [[0, 2], [-1, 2]] + G8, KL, 1.0, ["nb"], ["sK"])
+    put(T.sGn[:, 0:32], T.zero[:, 0:32], [[0, 4]] + G8, PA, -4096.0, ["zero"], ["sGa"])
+    put(T.sGn[:, 32:48], T.zero[:, 0:16], G8 + [[0, 2]], PA, -4096.0, ["zero"], ["sGb"])
+    put(T.nb2[:], T.zero[:, 0:16], G8 + [[0, 2]], 0, -1.0, ["zero"], ["nb2"])
+    put(T.sP[:, 0:16], T.nb[:, 0:16], [[0, 2]] + G8, IDB, 1.0, ["nb"], ["sP"])
+    fill(T.sP[:, 32:48], 16, 0, [], ["sP"])
+    put(T.sP[:, 16:32], T.nb2[:], G8 + [[0, 2]], IDB, 1.0, ["nb2"], ["sP"])
+    put(T.sP[:, 48:64], T.nb[:, 0:16], [[1, 2]] + G8, KR, 1.0, ["nb"], ["sP"])
+    for k in (T.UPT, T.UU):
+        fill(k[:, 0:SH], SH, 0, [], ["UPp"])
+        fill(k[:, NI:912], 912 - NI, 0, [], ["UPp"])
+    zcopy(KL)
+    zcopy(KR)
 
     def last_fills():
-        pick(T.sN[:, 0:16], T.onef[:, 0:16], [[-2, 2]] + G8, KL, ["sN"])
-        pick(T.sN[:, 16:32], T.onef[:, 0:16], [[2, 2]] + G8, KR, ["sN"])
-        pick(T.sN[:, 32:48], T.onef[:, 0:16], [[0, 2]] + G8, PA, ["sN"])
-        put(T.sN[:, 32:40], T.sN[:, 32:40], G8, PA, -1.0, ["sN"])
         fill(T.NT[:, 0:SH], SH, 0, [], ["NTp"])
-        fill(T.NT[:, SH + NI:912], 912 - SH - NI, NI, [], ["NTp"])
+        fill(T.NT[:, SH + NI:912], 912 - SH - NI, 0, [], ["NTp"])
+        put(T.sN[:, 0:16], T.zero[:, 0:16], [[0, 2]] + G8, SB, 1.0, ["zero"], ["sN0"])
+        put(T.sN[:, 16:32], T.zero[:, 0:16], [[-1, 2]] + G8, KL, 1.0, ["zero"], ["sN"])
+        put(T.sN[:, 32:48], T.zero[:, 0:16], [[1, 2]] + G8, KR, 1.0, ["zero"], ["sN"])
+        put(T.sN[:, 48:64], T.zero[:, 0:16], [[0, 2]] + G8, PA, 1.0, ["zero"], ["sN1"])
+        put(T.sN[:, 16:48], T.sN[:, 16:48], [[0, 2], [-1, 2]] + G8, MC, -4096.0, ["sN"], ["sN"])
+        fill(T.H2[:, NI:NI + SH], SH, 0, [], ["H2q"])
         for k in (1, 2):
             fill(H[k][:, 0:SH], SH, 0, [], ["H%dp" % k])
             fill(H[k][:, TW - 8:TW], 8, 0, [], ["H%dp" % k])
 
-    uk = ["UB", "u1", "u3", "u5", "u7", "u9", "u14", "u15"]
+    def gain_start(h):
+        op("P", mm(bank(D0 + h, 0, HB), T.crow[0:1], T.one[0:1, :], True, False), ["crow", "one", "one1"], pb(D0 + h))
+
+    def gain_sum(t, h):
+        op("P", mm(bank(D0 + h, 0, HB), T.Bp[:], H[t][:, SH + HB * h:SH + HB * h + HB]), ["Bp"] + hkeys(t)[2 * h:3 + 2 * h], pb(D0 + h))
+
+    for h in range(2):
+        gain_start(h)
+        gain_sum(0, h)
+    uk = ["UB", "u1", "u2", "u3", "u4", "u5", "u6", "u7"]
     for t in range(RO):
         last = t == RO - 1
         Ht, hk = H[t], hkeys(t)
         win = Ht[:]
-        for b in range(2):
-            a, e = BK[b]
-            op("P", mm(pD[b][:, 0:e - a], T.crow[0:1], T.one[0:1, 0:e - a], True, False), ["crow"], ["pD%d" % b])
-        for b in range(2):
-            a, e = BK[b]
-            op("P", mm(pD[b][:, 0:e - a], T.Bp[:], Ht[:, SH + a:SH + e]), ["Bp"] + hk[0:4], ["pD%d" % b])
-        for b in range(2):
-            op("P", unwrap(pD[b], b), uk, ["pD%d" % b])
-        op("P", tolist(0, T.ZS, ZK[PA], False, True) + tolist(1, T.ZS, ZK[IC], True), ["z2", "z3"], ["pW"])
         for c in range(4):
-            a, e = CH[c]
-            sc(T.AA[:, a:e], win.indirect(lst(SB, a, e)), hk + ["l7"], ["A%d" % c])
-        if t == 0:
-            late()
-        lv = [] if last else leaves(t + 1, T.pX, "pX")
-        for f in lv[0:1]:
-            f()
+            a, e = CG[c]
+            sc(T.AA[:, a:e], win.indirect(lst(SB, a, e)), hk + ["l3"], ["A%d" % c])
+            if c == 1 and t > 0:
+                sc(T.UB[0:UP, :, SB:PA + 1, :], T.pS[0:UP, :, 0:2, :], ["UB"], pb(BS) + ["u3", "u4"])
         for c in range(4):
-            a, e = CH[c]
-            b = c // 2
-            o = BK[b][0]
-            vt(T.M0[:, a:e], win.indirect(lst(KR, a, e)), T.AA[:, a:e], A.max, hk + ["l3", "A%d" % c], ["M0%d" % c])
+            a, e = CG[c]
+            h = c // 2
+            fb = (F0, F0, F1, BX)[c]
+            vt(T.M0[:, a:e], win.indirect(lst(KR, a, e)), T.AA[:, a:e], A.max, hk + ["l2", "A%d" % c], ["M0%d" % c])
             vt(T.M1[:, a:e], win.indirect(lst(KL, a, e)), T.AA[:, a:e], A.max, hk + ["l1", "A%d" % c], ["M1%d" % c])
-            op("P", [mm(pD[b][:, a - o:e - o], T.Bn[:], T.M0[:, a:e], False, c % 2 == 1),
-                     mm(pF[b][:, a - o:e - o], T.Bp[:], T.M0[:, a:e], True, False)], ["Bn", "Bp", "M0%d" % c], ["pD%d" % b, "pF%d" % b])
-            op("P", mm(pF[b][:, a - o:e - o], T.Bn[:], T.M1[:, a:e], False, True), ["M1%d" % c], ["pF%d" % b])
-            if c % 2 == 1:
-                op("S", lambda: S.activation(T.RR[:, o:e], pF[b][:, 0:e - o], F.Relu, bias=T.bias[:, 0:1]), ["bias0"], ["pF%d" % b, "RR%d" % b])
             if c == 1:
-                for f in lv[1:2]:
+                for j in range(2):
+                    op("P", unwrap(j, False), uk, pb(D0 + j))
+            op("P", [mm(bank(D0 + h, a - HB * h, e - HB * h), T.Bn[:], T.M0[:, a:e], False, c % 2 == 1),
+                     mm(bank(fb, a - HB * h, e - HB * h), T.Bp[:], T.M0[:, a:e], True, False)], ["Bn", "Bp", "M0%d" % c], pb(D0 + h, fb))
+            op("P", mm(bank(fb, a - HB * h, e - HB * h), T.Bn[:], T.M1[:, a:e], False, True), ["M1%d" % c], pb(fb))
+            if c == 0 and t == 0:
+                for f in leaves(1, BY):
                     f()
-                if t == 1:
-                    dma("Y", "o0", T.yh[:, NI:NI + NV], T.H3[:, NI:NI + NV], ["H3l"], [])
-        for b in range(2):
-            a, e = BK[b]
-            vt(T.T0[:, SH + a:SH + e], pD[b][:, 0:e - a], T.RR[:, a:e], A.add, ["RR%d" % b, "T0t"], ["pD%d" % b, "T0%d" % b])
-            if b == 0:
-                vs(T.lst[:, 4:6, :], T.pW[:, 0:112], SH, A.add, [], ["pW", "l9", "l11"])
+            if c == 1:
+                op("P", tolist(BW, 0, T.ZS, PA - 1, True) + [m for f in range(4 * (t > 0)) for m in tolist(BW, 0, T.ZP, f)] +
+                   tolist(BW, 1, T.ZS, IC - 1, False, True), ["z4", "z5", "ZP"], pb(BW))
+                if t > 0:
+                    zcopy(SB)
+                    zcopy(PA)
+            if c > 0:
+                a = 0 if c == 1 else a
+                op("S", lambda: S.activation(T.RR[:, a:e], bank(fb, a - HB * h, e - HB * h), F.Relu, bias=T.bias[:, 0:1]), ["bias0"],
+                   pb(fb) + ["RR%d" % c])
+        vt(T.T0[:, SH:SH + HB], bank(D0, 0, HB), T.RR[:, 0:HB], A.add, ["RR1", "T0t"], pb(D0) + ["T00"])
+        vt(T.T0[:, SH + HB:SH + NI], bank(D1, 0, HB), T.RR[:, HB:NI], A.add, ["RR2", "RR3", "T0t"], pb(D1) + ["T01"])
+        cast(PA, 2, BW)
         if t == 0:
-            vc(T.ZY[:], T.zero[:, 0:392], ["zero"], ["ZY"])
-            vc(T.ZX[:], T.zero[:, 0:520], ["zero"], ["ZX"])
-        tk = ["T00", "T01", "T0t"]
-        for c in range(4):
-            a, e = CQ[c]
-            op("S", lambda: S.activation(T.TT[:, a:e], T.T0[:].indirect(lst(KL, a, e)), F.Relu, bias=T.bias[:, 1:2]), tk + ["l1", "bias1"], ["TT%d" % c])
-            vt(T.KK[:, SH + a:SH + e], T.T0[:].indirect(lst(KR, a, e)), T.TT[:, a:e], A.max, tk + ["l3", "TT%d" % c], ["KK%d" % c])
-            if c < 2:
-                twin(T.K2[:, a:e], T.KK[:, SH + a:SH + e], e - a, "KK%d" % c, "K2%d" % c)
-        for c in (2, 3):
-            a, e = CQ[c]
-            sc(T.K2[:, a:e], T.KK[:, SH + a:SH + e], ["KK%d" % c], ["K2%d" % c])
-        kk, up, uu = four("KK") + ["KKp"], four("UP") + ["UPp"], four("UU") + ["UUp", "UUq"]
-        ny = 2 if last else 3
-        op("P", [const(T.pX, 0, -1, True), const(T.pX, 2, -1)] +
-           [mm(fld(T.pX, f), J2, ub((KL, KL, KR, KR)[f])) for f in range(4)] +
-           [mm(fld(T.pX, 4 + f), J1, ub((KR, KR, KL, KL)[f])) for f in range(4)], ["rows", "In1", "In2", "u1", "u3"], ["pX"])
-        op("P", [const(T.pY, 1, 1, True)] +
-           [mm(fld(T.pY, f), J1, ub((IDB, IDB, SB)[f])) for f in range(ny)] +
-           [mm(fld(T.pY, 4 + f), J1, ub((KL, KR, PA)[f])) for f in range(ny)] +
-           [mm(fld(T.pY, 4 + f), I1, ub(SB)) for f in range(ny)], ["u1", "u3", "u7", "u9", "u14"], ["pY"])
-        op("P", [mm(T.pS[0:UP, :, j, :], I1, ub((KL, KR, PA)[j]), j == 0) for j in range(ny)], ["u1", "u3", "u9"], ["pS"])
-        op("P", [m for j in range(ny) for m in tolist(j, T.ZS, j, False, j == 0)], ["z0", "z1", "z2"], ["pW"])
-        for c in range(4):
-            a, e = CQ[c]
-            vt(T.UPT[:, SH + a:SH + e], T.KK[:].indirect(lst(PA, a, e)), T.K2[:, a:e], A.is_lt, kk + ["K2%d" % c, "l9", "UPp"], ["UP%d" % c])
-            twin(T.U2[:, a:e], T.UPT[:, SH + a:SH + e], e - a, "UP%d" % c, "U2%d" % c)
-        sc(T.KP[:], T.KK[:].indirect(lst(PA)), kk + ["l9"], ["KP"])
-        op("P", wrap(T.KK, SH, T.sK[:], T.pX, 0, 8), kk + ["sK"], ["pX"])
-        for c in range(4):
-            a, e = CQ[c]
-            vt(T.UU[:, SH + a:SH + e], T.UPT[:].indirect(lst(SB, a, e)), T.U2[:, a:e], A.max, up + ["U2%d" % c, "l7", "UUp"], ["UU%d" % c])
-        sc(T.DD[:], T.UPT[:].indirect(lst(PA)), up + ["l9"], ["DD"])
-        op("P", wrap(T.KP, 0, T.sP[:, 0:8 * ny], T.pY, 0, ny), ["KP", "sP"], ["pY"])
-        op("P", wrap(T.UPT, SH, T.sGn[:], T.pX, 0, 4), up + ["sGn"], ["pX"])
-        vc(T.N1[:, 0:448], T.UU[:].indirect(lst(IC, 0, 448)), uu + ["l11"], ["N10"])
-        sc(T.N1[:, 448:NI], T.UU[:].indirect(lst(IC, 448, NI)), uu + ["l11"], ["N11"])
-        op("P", wrap(T.DD, 0, T.sGn[:, 0:8 * ny], T.pY, 0, ny), ["DD"], ["pY"])
-        op("P", wrap(T.UU, SH, T.sGp[:, 0:8 * ny], T.pY, 0, ny, True), uu + ["sGp"], ["pY"])
-        op("P", wrap(T.N1, 0, T.sGp[:], T.pX, 0, 4, True), ["N10", "N11"], ["pX"])
+            op("S", lambda: S.activation(T.bias[:, 1:2], T.bt[:, 25:26], F.Identity, bias=2048.0, scale=-2048.0), ["bt4"], ["bias1"])
+            op("S", lambda: S.activation(T.In1[:], T.Ib[:], F.Identity, scale=-1.0), ["Ib"], ["In1"])
+            op("S", lambda: S.activation(T.In2[:], T.Ib[:], F.Identity, scale=-2.0), ["Ib"], ["In2"])
+        tk = ["T00", "T01", "T0t", "T0u", "T0v"]
+        for c in range(5):
+            a, e = CK[c]
+            if c == 0:
+                op("V", lambda: V.tensor_scalar(T.TT[:, a:e], T.T0[:].indirect(lst(KL, a, e)), T.bias[:, 1:2], 0.0, A.add, A.max),
+                   tk + ["l1", "bias1"], ["TT0"])
+            else:
+                op("S", lambda: S.activation(T.TT[:, a:e], T.T0[:].indirect(lst(KL, a, e)), F.Relu, bias=T.bias[:, 1:2]),
+                   tk + ["l1", "bias1"], ["TT%d" % c])
+            vt(T.KK[:, SH + a:SH + e], T.T0[:].indirect(lst(KR, a, e)), T.TT[:, a:e], A.max, tk + ["l2", "TT%d" % c], ["KK%d" % c])
+            if 0 < c < 4:
+                a, e = CU[c - 1]
+                twin(T.K2[:, a:e], T.KK[:, SH + a:SH + e], e - a, ["KK0", "KK%d" % c], ["K2%d" % (c - 1)])
         if t == 0:
-            ghosts(2)
+            sc(T.idc[:], T.iv2[:], ["iv2"], ["idc"])
+            op("S", lambda: S.activation(T.sGp[:], T.sGn[:], F.Identity, scale=-1.0), ["sGa", "sGb"], ["sGp"])
+        sc(T.K2[:, CU[3][0]:NI], T.KK[:, SH + CU[3][0]:SH + NI], ["KK4"], ["K23"])
+        kk, up, uu = names("KK", 5) + ["KKp"], names("UP") + ["UPp", "UPr"], names("UU") + ["UPp", "UPr"]
+        op("P", [less1(fld(BX, 0), True), less1(fld(BX, 2))] +
+           [mm(fld(BX, f), J2, ub((KL, KL, KR, KR)[f])) for f in range(4)] +
+           [mm(fld(BX, 4 + f), J1, ub((KR, KR, KL, KL)[f])) for f in range(4)], ["rows", "In1", "In2", "u1", "u2"], pb(BX))
+        if not last:
+            op("P", [mm(fld(F0, 6 + f), I1, ub(PA), f == 0) for f in range(2)] + [mm(fld(F0, 6 + f), J1, ub(SB), False, f == 1) for f in range(2)],
+               ["u3", "u4"], pb(F0))
+            op("P", [mm(fld(F1, f), J1, ub((SB, SB, ID, ID, ID, ID, PA, PA)[f]), f == 0) for f in range(8)], ["u3", "u4", "u5"], pb(F1))
+        op("P", tolist(BW, 0, T.ZS, 0, True) + tolist(BW, 1, T.ZS, 1), ["z1", "z2"], pb(BW))
+        op("P", [mm(st(j), I1, ub(KL + j), j == 0) for j in range(2)], ["u1", "u2"], pb(BS))
+        op("P", wrap(T.KK, SH, T.sK[:], BX, 8), kk + ["sK"], pb(BX))
+        op("P", [less1(fld(BY, 0), True), mm(fld(BY, 2, 2), J1, T.idc[0:UP])] +
+           [mm(fld(BY, f), (J2, J2, None, None, I1, I1, J1, J1)[f], ub(SB)) for f in (0, 1, 4, 5, 6, 7)] +
+           [mm(fld(BY, 4 + f), J1, ub(KL + f)) for f in range(2)], ["u3", "idc"], pb(BY))
+        if last:
+            lv = leaves(t, D0)
+        for c in range(4):
+            a, e = CU[c]
+            vt(T.UPT[:, SH + a:SH + e], T.KK[:].indirect(lst(PA, a, e)), T.K2[:, a:e], A.is_lt, kk + ["K2%d" % c, "l4", "UPp"], ["UP%d" % c])
+            if c < 3:
+                twin(T.U2[:, a:e], T.UPT[:, SH + a:SH + e], e - a, ["UP%d" % c], ["U2%d" % c])
+        sc(T.KP[:], T.KK[:].indirect(lst(PA)), kk + ["l4"], ["KP"])
+        op("P", wrap(T.KP, 0, T.sP[:], BY, 8), ["KP", "sP"], pb(BY))
+        op("P", wrap(T.UPT, SH, T.sGn[:, 0:32], BX, 4), up + ["sGa", "sGb"], pb(BX))
+        vc(T.U2[:, CU[3][0]:NI], T.UPT[:, SH + CU[3][0]:SH + NI], ["UP3"], ["U23"])
+        for c in range(4):
+            a, e = CU[c]
+            vt(T.UU[:, SH + a:SH + e], T.UPT[:].indirect(lst(SB, a, e)), T.U2[:, a:e], A.max, up + ["U2%d" % c, "l3"], ["UU%d" % c])
+        sc(T.DD[:], T.UPT[:].indirect(lst(PA)), up + ["l4"], ["DD"])
+        op("P", wrap(T.DD, 0, T.sGn[:, 16:48], BY, 4), ["DD"], pb(BY))
+        op("P", wrap(T.UU, SH, T.sGp[:, 16:48], BY, 4, True), uu + ["sGp"], pb(BY))
+        nv = N1V if last else N1A
+        vc(T.N1[:, 0:nv], T.UU[:].indirect(lst(IC, 0, nv)), uu + ["l5"], ["N10"])
+        sc(T.N1[:, N1V:NI], T.UU[:].indirect(lst(IC, N1V, NI)), uu + ["l5"], ["N11"])
+        if t == 0:
             last_fills()
-            send(2)
-        vs(T.EY[0:UP, 0:64 * ny], fld(T.pY, 0, ny), -4096.0, A.is_equal, [], ["pY", "EY"])
-        vt(zf(T.ZY, 0, ny), fld(T.pY, 4, ny), T.EY[0:UP, 0:64 * ny], A.mult, ["EY", "ZY"], ["pY", "ZY"])
-        op("P", [m for f in range(ny) for m in tolist(f, T.ZY, f)], ["ZY"], ["pW"])
-        op("P", [mm(T.pS[0:UP, :, f, :], I1, zf(T.ZY, f)) for f in range(ny)], ["ZY"], ["pS"])
-        vs(T.EQ[0:UP], fld(T.pX, 0, 4), -4096.0, A.is_equal, [], ["pX", "EQ"])
-        vt(zf(T.ZX, 0, 4), fld(T.pX, 4, 4), T.EQ[0:UP], A.mult, ["EQ", "ZX"], ["pX", "ZX"])
+        if last:
+            for f in lv:
+                f()
+            dma("Y", "o0", [(T.yh[:, NI:NI + NV], T.H3[:, NI:NI + NV])], ["H3l"], [])
+        vs(T.UB[0:UP, :, MC:MD + 1, :], fld(BY, 2, 2), -4096.0, A.is_equal, ["UB"], pb(BY) + ["u7"])
+        if not last:
+            op("P", unwrap(0, True), uk, pb(D0))
+            vc(T.N1[:, nv:N1V], T.UU[:].indirect(lst(IC, nv, N1V)), uu + ["l5"], ["N12"])
+        op("P", wrap(T.N1, 0, T.sGp[:, 0:32], BX, 4, True), ["N10", "N11", "N12"], pb(BX))
+        for f in range(2):
+            vt(zf(T.ZY, 2 + f), fld(BY, 4 + f), ub(MC + f), A.mult, ["u7", "ZY"], pb(BY) + ["ZYu"])
+        if not last:
+            op("P", unwrap(1, True), uk, pb(D1))
+            vs(T.MK[0:UP, 2, :], fld(BY, 0, 2), -4096.0, A.is_equal, [], pb(BY) + ["MK1"])
+            for h in range(2):
+                sc(T.NT[:, SH + HB * h:SH + HB * h + HB], bank(D0 + h, 0, HB), [], pb(D0 + h) + ["NT%d" % h])
+        op("P", [m for f in range(2) for m in tolist(BW, f, T.ZY, 2 + f)], ["ZYu"], pb(BW))
+        op("P", [mm(st(f), I1, zf(T.ZY, 2 + f)) for f in range(2)], ["ZYu"], pb(BS))
+        vs(T.EQ[0:UP], fld(BX, 0, 4), -4096.0, A.is_equal, [], pb(BX) + ["EQ"])
+        vt(zf(T.ZX, 0, 4), fld(BX, 4, 4), T.EQ[0:UP], A.mult, ["EQ", "ZX"], pb(BX) + ["ZX"])
+        op("P", [m for f in range(4) for m in tolist(BW, 1 - f // 2, T.ZX, f, False, f == 3)], ["ZX"], pb(BW))
+        op("P", [mm(st(1 - f // 2), I1, zf(T.ZX, f), False, f == 3) for f in range(4)], ["ZX"], pb(BS))
+        if not last:
+            vt(zf(T.ZY, 0, 2), fld(BY, 6, 2), T.MK[0:UP, 2, :], A.mult, ["MK1", "ZY"], pb(BY) + ["ZYw"])
+        vs(T.lst[:, 0:2, :], bank(BW, 0, 112), SH, A.add, [], pb(BW) + ["l1", "l2"])
 
-        def lists():
-            op("P", [m for f in range(4) for m in tolist(1 - f // 2, T.ZX, f, f == 3)], ["ZX"], ["pW"])
-
-        def state():
-            op("P", [mm(T.pS[0:UP, :, 1 - f // 2, :], I1, zf(T.ZX, f), False, f == 3) for f in range(4)], ["ZX"], ["pS"])
-
-        def vlists():
-            vs(T.lst[:, 0:ny, :], T.pW[:, 0:56 * ny], SH, A.add, [], ["pW", "l1", "l3", "l5"])
-
-        def vstate():
-            vc(T.UB[0:UP, :, KL:2 * ny:2, :], T.pS[0:UP, :, 0:ny, :], ["UB"], ["pS", "u1", "u3", "u5"])
-
-        for f in ((lists, state, vlists, vstate) if last else (state, lists, vstate, vlists)):
-            f()
-        op("P", unwrap(pF[0], 0, True, True), uk, ["pF0"])
-        op("P", unwrap(pF[1], 1, True, True), uk, ["pF1"])
+        CN = CO if last else CK
 
         def newc(c):
-            a, e = CQ[c]
-            sc(T.BB[:, a:e], win.indirect(lst(KL, a, e)), hk + ["l1"], ["B%d" % c])
+            a, e = CN[c]
+            (sc if c else vc)(T.BB[:, a:e], win.indirect(lst(KL, a, e)), hk + ["l1"], ["B%d" % c])
 
         def newm(c):
-            a, e = CQ[c]
+            a, e = CN[c]
             out = T.H3[:, a:e] if last else H[t + 1][:, SH + a:SH + e]
-            vt(out, win.indirect(lst(KR, a, e)), T.BB[:, a:e], A.max, hk + ["l3", "B%d" % c], ["H%d_%d" % (t + 1, c)])
+            vt(out, win.indirect(lst(KR, a, e)), T.BB[:, a:e], A.max, hk + ["l2", "B%d" % c], ["H%d_%d" % (t + 1, c)] + ["H%dq" % (t + 1)] * (c == 4))
 
         if not last:
-            nt = ["NT0", "NT1", "NTp", "l5"]
-            op("P", [mm(fld(T.pX, f), J1, ub(ID), f == 0) for f in (0, 1)] + [mm(fld(T.pX, f), J1, ub(PP)) for f in (2, 3)] +
-               [mm(fld(T.pX, 4), I1, ub(PP)), const(T.pX, 5, 0)], ["u15", "u5"], ["pX"])
-            op("P", mm(T.pS[0:UP, :, 3, :], I1, ub(PP), True), ["u5"], ["pS"])
-            op("P", tolist(0, T.ZS, ZK[PA], False, True) + tolist(0, T.ZY, 2), ["z2", "ZY"], ["pW"])
-            newc(0)
-            vt(zf(T.ZS, ZK[IC]), ub(KL), ub(KR), A.min, ["u1", "u3", "ZS"], ["z3"])
-            vc(T.NT[:, SH:SH + 512], pF[0][:, 0:512], [], ["pF0", "NT0"])
-            sc(T.NT[:, SH + 512:SH + NI], pF[1][:, 0:384], [], ["pF1", "NT1"])
-            vc(T.NP[:, 0:448], T.NT[:].indirect(lst(PP, 0, 448)), nt, ["NP0"])
-            sc(T.NP[:, 448:NI], T.NT[:].indirect(lst(PP, 448, NI)), nt, ["NP1"])
-            op("P", wrap(T.NP, 0, T.sN[:], T.pX, 0, 6, True), ["NP0", "NP1", "sN"], ["pX"])
-            for c in range(1, 4):
+            nt = ["NT0", "NT1", "NTp", "l4"]
+            sc(T.NP[:, 0:NPS], T.NT[:].indirect(lst(PA, 0, NPS)), nt, ["NP0"])
+            vc(T.NP[:, NPS:NI], T.NT[:].indirect(lst(PA, NPS, NI)), nt, ["NP1"])
+            op("P", tolist(BX, 0, T.ZS, SB - 1, True) + [m for f in range(4) for m in tolist(BX, 0, T.ZY, f, eye=T.Ih if f < 2 else T.In1)],
+               ["z3", "ZYu", "ZYw"], pb(BX))
+            op("P", [mm(fld(BW, f), I1, ub(SB), f == 0) for f in range(2)] + [mm(fld(BW, f), J1, ub(PA), False, f == 1) for f in range(2)],
+               ["u3", "u4"], pb(BW))
+            op("P", wrap(T.NP, 0, T.sN[:], F1, 8, True), ["NP0", "NP1", "sN", "sN0", "sN1"], pb(F1))
+            for h in range(2):
+                gain_start(h)
+            for c in range(5):
                 newc(c)
+            sc(T.UB[0:UP, :, KL:KR + 1, :], T.pS[0:UP, :, 0:2, :], ["UB"], pb(BS) + ["u1", "u2"])
+            zcopy(KL)
+            zcopy(KR)
             newm(0)
-            for j in range(2):
-                vc(zf(T.ZS, j), ub((KL, KR)[j]), ["u1", "u3", "ZS"], ["z%d" % j])
             newm(1)
+            vs(T.MK[0:UP, 0:2, :], fld(F1, 2, 4), -4096.0, A.is_equal, [], pb(F1) + ["MK0"])
             newm(2)
-            vs(T.EQ[0:UP, 0:128], fld(T.pX, 0, 2), 0.0, A.is_equal, [], ["pX", "EQ"])
-            vt(zf(T.ZX, 0, 2), fld(T.pX, 2, 2), T.EQ[0:UP, 0:128], A.mult, ["EQ", "ZX"], ["pX", "ZX"])
-            op("P", tolist(0, T.ZX, 0) + tolist(0, T.ZX, 1, True), ["ZX"], ["pW"])
-            op("P", [mm(T.pS[0:UP, :, 3, :], I1, zf(T.ZX, f), False, f == 1) for f in range(2)], ["ZX"], ["pS"])
-            vt(T.EY[0:UP, 0:64], T.EQ[0:UP, 0:64], T.EQ[0:UP, 64:128], A.add, ["EQ"], ["EY"])
+            vt(zf(T.ZX, 0, 4), fld(F0, 6, 4), T.MK[0:UP, 0:2, :], A.mult, ["MK0", "ZX"], pb(F0, F1) + ["ZX"])
+            op("P", [m for f in range(4) for m in tolist(BX, 0, T.ZX, f, False, f == 3)], ["ZX"], pb(BX))
             newm(3)
-            vs(lst(SB), T.pW[:, 0:56], SH, A.add, [], ["pW", "l7"])
-            vt(T.EY[0:UP, 64:128], fld(T.pX, 4), T.EY[0:UP, 0:64], A.mult, ["EY"], ["pX", "EY1"])
-            vc(ub(SB), T.pS[0:UP, :, 3, :], ["UB"], ["pS", "u7"])
-            vt(ub(PA), fld(T.pX, 5), T.EY[0:UP, 64:128], A.add, ["EY1", "UB"], ["pX", "u9"])
-            vc(zf(T.ZS, ZK[PA]), ub(PA), ["u9", "ZS"], ["z2"])
+            newm(4)
+            if t == 0:
+                ghosts(2)
+                send(2)
+            cast(SB, 1, BX)
+            op("P", [mm(st(j), I1, ub(SB + j), j == 0) for j in range(2)] + [mm(st(0), I1 if f < 2 else J1, zf(T.ZY, f)) for f in range(4)] +
+               [mm(st(0), I1, zf(T.ZX, f)) for f in range(4)], ["u3", "u4", "ZYu", "ZYw", "ZX"], pb(BS))
+            for h in range(2):
+                gain_sum(t + 1, h)
+            vt(zf(T.ZP, 0, 4), fld(F1, 6, 4), T.MK[0:UP, 0:3:2, :], A.mult, ["MK0", "MK1", "ZP"], pb(F1, BW) + ["ZP"])
+            vt(zf(T.ZS, IC - 1), ub(KL), ub(KR), A.min, ["u1", "u2", "ZS"], ["z5"])
+            op("P", [mm(st(1), I1, zf(T.ZP, f), False, f == 3) for f in range(4)], ["ZP"], pb(BS))
         else:
-            for c in range(4):
-                a, e = CQ[c]
-                newc(c)
+            newc(0)
+            vc(T.UK[0:UP, 16:144:8, :], T.pS[0:UP, :, 0:2, :], ["UK"], pb(BS) + ["uk"])
+            op("P", [mm(T.PS[:, 512 * F0 + r:512 * F0 + 224:8], T.UK[0:UP, 16 - 2 * j:144 - 2 * j, r], T.Ih[0:UP, 28 * j:28 * j + 28],
+                        r + j == 0, r + j == 10) for r in range(8) for j in range(4)], ["uk", "UK"], pb(F0))
+            for c in range(5):
+                a, e = CN[c]
+                if c > 0:
+                    newc(c)
                 newm(c)
                 if c > 0:
                     a = 0 if c == 1 else a
-                    dma("Y", "o%d" % c, T.yh[:, a:e], T.H3[:, a:e], ["H3_0", "H3_%d" % c], [])
-            sc(T.NT[:, SH:SH + 512], pF[0][:, 0:512], [], ["pF0", "NT0"])
-            sc(T.NT[:, SH + 512:SH + NI], pF[1][:, 0:384], [], ["pF1", "NT1"])
-            dma("S", "o4", T.yk[:, 0:NI], T.NT[KL::16, SH:SH + NI], ["NT0", "NT1"], [])
-            dma("Y", "o5", T.yk[:, NI:2 * NI], T.NT[KR::16, SH:SH + NI], ["NT0", "NT1"], [])
+                    dma("Y", "o%d" % c, [(T.yh[:, a:e], T.H3[:, a:e])], ["H3_0", "H3_%d" % c], [])
+            sc(T.NK[:], bank(F0, 0, 224), [], pb(F0) + ["NK"])
+            dma("S", "o5", [(T.yk[:], T.NK[0:128:2, :])], ["NK"], [])
 
     for s in top:
         need("G", (s, top[s]))

from concourse.bass import DstId, RemoteDMATransfer
from concourse.mybir import AluOpType, ActivationFunctionType, AxisListType

A, F = AluOpType, ActivationFunctionType
NI, NV, NG, RO = 896, 449, 64, 3
SH = 7
TW = 1808
GH = NI + NV + SH
NO = 2 * NI + 1
UP = 112
HB = NI // 2
KL, KR, SB, PA, ID, IDB, MC, MD = 1, 2, 3, 4, 5, 6, 7, 8
IC = 5
RND = 12582912.0
CG = [(0, 128), (128, 448), (448, 768), (768, 896)]
CK = [(0, 96), (96, 288), (288, 480), (480, 704), (704, 896)]
CU = [(0, 288), (288, 480), (480, 704), (704, 896)]
CO = [(0, 96), (96, 320), (320, 544), (544, 768), (768, 896)]
N1A, N1V, NPS = 224, 448, 672
BX, BY, D0, D1, F0, F1, BW, BS = range(8)
F32, F16, B16 = "float32", "float16", "bfloat16"

SCRATCH = {"kks": ("sbuf", [128, 2, 56], "int32"), "lst": ("sbuf", [128, 5, 56], "uint16"), "slu": ("sbuf", [128, 28], "uint16"),
           "UB": ("sbuf", [128, 8, 16, 8], F16), "UK": ("sbuf", [128, 144, 8], F16), "ZX": ("sbuf", [128, 81, 8], F16),
           "ZY": ("sbuf", [128, 65, 8], F16), "ZP": ("sbuf", [128, 65, 8], F16), "ZS": ("sbuf", [128, 81, 8], F16),
           "WP": ("sbuf", [128, 2, 2, UP], F16), "Ih3": ("sbuf", [128, 8, 16], F16), "MK": ("sbuf", [128, 3, 128], F32),
           "sW": ("sbuf", [128, 2, 16], F32), "crow": ("sbuf", [128, 8, 16], B16),
           "PS": ("psum", [128, 7 * 512], F32), "pS": ("psum", [128, 8, 8, 8], F32)}
for _dt, _bufs in (("int32", dict(h0s=1352, vels=452, sls=28)),
                   (B16, dict(velb=456, H0=TW, H1=TW, H2=TW, sb0=448, sb1=448, sb2=448, AA=NI, BB=NI, M0=NI, M1=NI, UPT=TW, UU=TW,
                              U2=NI, DD=NI, N1=NI, one=HB, Ib=128, Bp=128, Bn=128, sGp=48, sGn=48, sN=64, zero=648, rows=64)),
                   (F32, dict(LZ=452, H3=1348, vals=NI, W1=TW, W2=TW, RR=NI, T0=TW, TT=NI, KK=912, K2=NI, KP=NI, NT=912, NK=224,
                              EQ=256, onef=16, cw=16, nb=64, nb2=16, sK=64, sP=64, iv=64, iv2=128, bt=32, bias=4)),
                   (F16, dict(Ih=128, In1=128, In2=128, idc=128, NP=NI))):
    for _k in _bufs:
        SCRATCH[_k] = ("sbuf", [128, _bufs[_k]], _dt)
SEMAPHORES = ["cV", "cS", "cP", "cG", "dsl", "dlf", "dkl", "dkr", "dhi", "dve", "arr0", "arr1", "arr2", "sent",
              "f0", "f1", "f2", "f3", "o0", "o1", "o2", "o3", "o4", "o5"]


def rank_program(g, core, T, topo):
    rank = T.rank_of(core)
    if rank is None:
        return
    N = len(T.cores)
    Q = {"V": g.vector, "S": g.scalar, "P": g.tensor, "G": g, "Y": g.sync}
    cnt = {"V": 0, "S": 0, "P": 0, "G": 0}
    seen = {e: {} for e in Q}
    wr, rd, top = {}, {}, {}

    def need(e, tok):
        if seen[e].get(tok[0], 0) < tok[1]:
            Q[e].wait_ge(T.sem[tok[0]], tok[1])
            seen[e][tok[0]] = tok[1]

    def order(e, r, w):
        own = "c" + e
        toks = {}
        for k in r:
            if k in wr:
                toks[wr[k][0]] = max(toks.get(wr[k][0], 0), wr[k][1])
        for k in w:
            for t in rd.get(k, []) + ([wr[k]] if k in wr else []):
                if t[0] != own:
                    toks[t[0]] = max(toks.get(t[0], 0), t[1])
        for s in toks:
            need(e, (s, toks[s]))

    def note(tok, r, w):
        top[tok[0]] = tok[1]
        for k in r:
            rd.setdefault(k, []).append(tok)
        for k in w:
            wr[k] = tok
            rd[k] = []

    def op(e, fns, r, w):
        order(e, r, w)
        if not isinstance(fns, list):
            fns = [fns]
        for f in fns:
            ins = f()
        cnt[e] += 1
        ins.then_inc(T.sem["c" + e], 1)
        note(("c" + e, cnt[e]), r, w)

    def dma(e, sem, pairs, r, w):
        order(e, r, w)
        for out, in_ in pairs:
            Q[e].dma_start(out, in_).then_inc(T.sem[sem], 16)
        note((sem, top.get(sem, 0) + 16 * len(pairs)), r, w)

    V, S, P = g.vector, g.scalar, g.tensor
    H = [T.H0, T.H1, T.H2, T.H3]
    I1, J1, J2 = T.Ih[0:UP, 0:UP], T.In1[0:UP, 0:UP], T.In2[0:UP, 0:UP]

    def vc(out, in_, r, w):
        op("V", lambda: V.tensor_copy(out, in_), r, w)

    def vt(out, a, b, o, r, w):
        op("V", lambda: V.tensor_tensor(out, a, b, o), r, w)

    def vs(out, a, s, o, r, w):
        op("V", lambda: V.tensor_scalar(out, a, s, None, o), r, w)

    def sc(out, in_, r, w):
        op("S", lambda: S.activation(out, in_, F.Copy), r, w)

    def names(k, n=4):
        return ["%s%d" % (k, c) for c in range(n)]

    def pb(*banks):
        return ["p%d" % b for b in banks]

    def bank(b, a, e, parts=128):
        return T.PS[0:parts, 512 * b + a:512 * b + e]

    def fld(b, f, n=1):
        return bank(b, 64 * f, 64 * (f + n), UP)

    def lst(t, a=0, b=NI):
        return T.lst[:, t - 1, a // 16:b // 16]

    def ub(t):
        return T.UB[0:UP, :, t, :]

    def zf(Z, f, n=1):
        return Z[0:UP, 16 * f + 1:16 * (f + n):2, :]

    def hkeys(t):
        return names("H%d_" % t, 5) + ["H%dl" % t, "H%dg" % t, "H%dp" % t]

    def mm(out, lhsT, rhs, start=False, stop=False):
        return lambda: P.matmul(out, lhsT, rhs, start, stop)

    def less1(out, start=False):
        return mm(out, T.one[0:1, 0:UP], T.rows[0:1, :], start)

    def wrap(tab, off, rhs, b, nf, stop=False, start=False):
        return [mm(T.PS[0:UP, 512 * b + r:512 * b + 64 * nf:8], tab[:, off + r:off + NI:8], rhs, start and r == 0, stop and r == 7)
                for r in range(8)]

    def unwrap(h, alone):
        b = D0 + h
        return [mm(T.PS[:, 512 * b + r:512 * b + HB:8], T.UB[0:UP, :, :, r], T.Ih[0:UP, 56 * h:56 * h + 56], alone, alone) for r in range(8)]

    def tolist(b, j, Z, f, start=False, stop=False, eye=T.Ih):
        return [mm(bank(b, 56 * j, 56 * j + 56), Z[0:UP, 16 * f + 1 - h:16 * f + 17 - h, :], eye[0:UP, h:UP:2],
                   start and h == 0, stop and h == 1) for h in range(2)]

    def cast(t, n, b):
        op("S", lambda: S.activation(T.lst[:, t - 1:t - 1 + n, :], bank(b, 0, 56 * n), F.Identity, bias=float(SH)), [],
           pb(b) + ["l%d" % (t + j) for j in range(n)])

    def st(j):
        return T.pS[0:UP, :, j, :]

    def fill(out, n, val, r, w):
        op("G", lambda: g.iota(out, [[0, n]], val, 0, allow_small_or_imprecise_dtypes=True), r, w)

    def pick(out, src, pat, t, r, w):
        op("G", lambda: g.affine_select(out, src, pat, A.is_equal, 0.0, -t, 1), r, w)

    def put(out, src, pat, t, val, r, w):
        op("G", lambda: g.affine_select(out, src, pat, A.not_equal, val, -t, 1), r, w)

    def twin(out, src, n, r, w):
        op("G", lambda: g.affine_select(out, src, [[0, n]], A.is_ge, 0.0, 0, 0), r, w)

    def send(t):
        trs = []
        for d in range(1, N):
            dst = T.cores[(rank + d) % N]
            rid, pid = topo.addr(dst, core)
            trs.append(RemoteDMATransfer(dst_ids=[DstId(rid=rid, pnc=pid)], dma_engine_mask=1 << topo.engines(core, dst)[d - 1],
                                         remote_sem=T.sem["arr%d" % t], src=T["sb%d" % t][:, NG * (d - 1):NG * d],
                                         dst=H[t][:, GH + NG * (d - 1):GH + NG * d]))
        order("G", ["sb%d" % t], [])
        g.remote_dma_fused(trs, local_sem=T.sem.sent)
        top["sent"] = top.get("sent", 0) + N - 1

    def leaves(t, b):
        ps = bank(b, 0, NV)
        op("P", [mm(ps, T.Ib[:], H[t][:, NI + SH:GH], True, False), mm(ps, T.Ib[:], T.velb[:, 0:NV], False, True)],
           ["Ib", "H%dl" % t, "velb"], pb(b))
        out = T.H3[:, NI:NI + NV] if t == RO - 1 else H[t + 1][:, NI + SH:GH]
        return [lambda: op("S", lambda: S.activation(T.LZ[:, 0:NV], ps, F.Relu, bias=255.0, scale=-1.0), [], pb(b) + ["LZ"]),
                lambda: op("S", lambda: S.activation(out, T.LZ[:, 0:NV], F.Relu, bias=255.0, scale=-1.0), ["LZ"], ["H%dl" % (t + 1)])]

    def ghosts(t):
        sc(T["sb%d" % t][:], H[t][:, NI:GH].indirect(T.slu[:]), ["slu", "H%dl" % t, "H%dq" % t], ["sb%d" % t])

    for t in range(RO):
        wr["H%dg" % t] = ("arr%d" % t, N - 1)
        top["arr%d" % t] = N - 1

    dma("Y", "dkl", [(T.kks[:, 0, :], T.kl[:])], [], ["kk0"])
    dma("S", "dkr", [(T.kks[:, 1, :], T.kr[:])], [], ["kk1"])
    dma("Y", "dlf", [(T.h0s[:, NI:GH], T.h0[:, NI - SH:NI + NV])], [], ["h0l"])
    dma("S", "dsl", [(T.sls[:], T.sl[:])], [], ["sls"])
    dma("Y", "dve", [(T.vels[:, 0:NV], T.vel[:])], [], ["vels"])
    dma("Y", "dhi", [(T.h0s[:, SH:NI], T.h0[:, 0:NI - SH])], [], ["h0i"])

    G8 = [[-16, 8]]
    op("V", lambda: V.memset(T.one[:, 0:128], 1.0), [], ["one"])
    op("V", lambda: V.memset(T.zero[:], 0.0), [], ["zero"])
    op("G", lambda: g.iota(T.iv[:], [[0, 8], [1, 8]], 0, 8, allow_small_or_imprecise_dtypes=True), [], ["iv"])
    op("G", lambda: g.affine_select(T.Ib[:], T.one[:, 0:128], [[-1, 128]], A.is_equal, 0.0, 0, 1), ["one"], ["Ib"])
    op("S", lambda: S.activation(T.W1[:, 0:64], T.one[:, 0:64], F.Silu, scale=0.0), ["one"], ["W1"])
    sc(T.W1[:, 64:512], T.zero[:, 0:448], ["zero"], ["W1"])
    sc(T.W1[:, 512:904], T.zero[:, 0:392], ["zero"], ["W1"])
    op("V", lambda: V.memset(T.onef[:], 1.0), [], ["onef"])
    op("V", lambda: V.memset(T.cw[:], -1.0 / 32), [], ["cw"])
    vc(T.WP[:], T.zero[:, 0:448], ["zero"], ["WP"])
    for j in range(2):
        vc(T.UB[:, 4 * j:4 * j + 4], T.zero[:, 0:512], ["zero"], ["UB"])
    pick(T.bt[:, 0:8], T.onef[:, 0:8], G8, ID, ["onef"], ["bt0"])
    fill(T.W2[:, 0:904], 904, 0, [], ["W2"])
    vc(T.Ih3[:], T.Ib[:], ["Ib"], ["Ih3"])
    vc(T.Ih[:], T.Ib[:], ["Ib"], ["Ih"])
    vc(ub(ID), T.iv[0:UP], ["iv", "UB"], ["u5"])
    pick(T.sW[:, 0, 0:8], T.cw[:, 0:8], G8, KR, ["cw"], ["sW0"])
    pick(T.sW[:, 0, 8:16], T.cw[:, 0:8], G8, ID, ["cw"], ["sW0"])
    pick(T.sW[:, 1, 0:8], T.cw[:, 0:8], G8, KL, ["cw"], ["sW1"])
    pick(T.sW[:, 1, 8:16], T.cw[:, 0:8], G8, ID, ["cw"], ["sW1"])
    dma("Y", "f0", [(T[k][:, a:a + 448], T.zero[:, 0:448]) for k in ("UPT", "UU") for a in (912, 1360)], ["zero", "h0l"], ["UPr"])
    sc(T.ZX[:], T.zero[:], ["zero"], ["ZX"])
    dma("Y", "f1", [(T.ZS[:], T.ZX[:])], ["ZX"], ["ZS"])
    dma("Y", "f2", [(T.ZY[:], T.ZX[:, 0:65]), (T.ZP[:], T.ZX[:, 0:65]), (T.UK[:, 0:72], T.ZX[:, 0:72]), (T.UK[:, 72:144], T.ZX[:, 0:72])],
        ["ZX"], ["ZY", "ZP", "UK"])

    for h in range(2):
        vc(T.WP[:, :, h, h:UP:2], T.kks[:], ["kk0", "kk1", "WP"], ["WP%d" % h])
    op("P", [mm(st(j), T.WP[:, j, h, :], T.Ih3[:, :, 8 * h:8 * h + 8], j + h == 0, j + h == 2) for j in range(2) for h in range(2)],
       ["WP0", "WP1", "Ih3"], pb(BS))
    vs(T.slu[:], T.sls[:], SH, A.add, ["sls"], ["slu"])
    op("V", lambda: V.tensor_reduce(T.bt[:, 24:25], T.bt[:, 0:8], AxisListType.X, A.add), ["bt0"], ["bt3"])
    vc(T.UB[0:UP, :, KL:KR + 1, :], T.pS[0:UP, :, 0:2, :], ["UB"], pb(BS) + ["u1", "u2"])
    for h in range(2):
        op("P", unwrap(h, True), ["UB", "u1", "u2", "u5", "Ih"], pb(D0 + h))
    op("V", lambda: V.tensor_scalar(T.bias[:, 2:3], T.bt[:, 24:25], 32.0 * (NI - NO), 32.0 * NO, A.mult, A.add), ["bt3"], ["bias2"])
    vs(T.lst[:, 0:2, :], T.kks[:], SH, A.add, ["kk0", "kk1"], ["l1", "l2"])
    sc(T.sb0[:], T.h0s[:, NI:GH].indirect(T.slu[:]), ["slu", "h0l"], ["sb0"])
    send(0)
    op("V", lambda: V.tensor_scalar(T.vals[:, 0:HB], bank(D0, 0, HB), -32.0, T.bias[:, 2:3], A.mult, A.add), ["bias2"], pb(D0) + ["vals0"])
    op("S", lambda: S.activation(T.vals[:, HB:NI], bank(D1, 0, HB), F.Identity, bias=T.bias[:, 2:3], scale=-32.0), ["bias2"], pb(D1) + ["vals1"])
    vc(T.W1[:].indirect(lst(KL, 0, HB)), T.vals[:, 0:HB], ["vals0", "l1", "W1"], ["W1"])
    vc(T.W1[:].indirect(lst(KL, HB, NI)), T.vals[:, HB:NI], ["vals1", "l1", "W1"], ["W1"])
    op("S", lambda: S.activation(T.W2[:].indirect(lst(KR)), T.vals[:], F.Silu), ["vals0", "vals1", "l2", "W2"], ["W2"])

    fill(T.H1[:, NI:NI + SH], SH, 0, [], ["H1q"])
    fill(T.H0[:, 0:SH], SH, 0, [], ["H0p"])
    fill(T.H0[:, TW - 8:TW], 8, 0, [], ["H0p"])
    fill(T.Bp[:], 128, 4096, [], ["Bp"])
    fill(T.crow[:], 128, -4096, [], ["crow"])
    op("G", lambda: g.affine_select(T.Bp[:], T.Bp[:], [[-16, 8], [0, 16]], A.is_ge, 0.0, 0, 1), ["Bp"], ["Bp"])
    fill(T.crow[:, :, PA], 8, -2048, ["crow"], ["crow"])
    op("G", lambda: g.affine_select(T.Bp[:], T.Bp[:], [[16, 8], [0, 16]], A.is_ge, 0.0, 15, -1), ["Bp"], ["Bp"])
    pick(T.bt[:, 8:16], T.onef[:, 0:8], G8, IDB, ["onef"], ["bt1"])
    pick(T.bt[:, 16:24], T.onef[:, 0:8], G8, PA, ["onef"], ["bt2"])
    fill(T.T0[:, 904:1356], 452, -4096, [], ["T0u"])
    dma("Y", "f3", [(T.T0[:, 1356:TW], T.T0[:, 904:1356])], ["T0u"], ["T0v"])

    op("P", wrap(T.W1, SH, T.sW[:, 0, :], BX, 2, False, True), ["W1", "sW0"], pb(BX))
    op("P", wrap(T.W2, SH, T.sW[:, 1, :], BX, 2, True), ["W2", "sW1"], pb(BX))
    vt(T.LZ[:, 0:NV], T.h0s[:, NI + SH:GH], T.vels[:, 0:NV], A.add, ["h0l", "vels"], ["LZ"])
    sc(T.H0[:, SH:SH + NI], T.h0s[:, SH:SH + NI], ["h0i", "h0l"], names("H0_", 5))
    vc(T.H0[:, NI + SH:GH], T.h0s[:, NI + SH:GH], ["h0l"], ["H0l"])
    op("V", lambda: V.tensor_scalar(T.H1[:, NI + SH:GH], T.LZ[:, 0:NV], 0.0, 255.0, A.max, A.min), ["LZ"], ["H1l"])
    sc(T.velb[:, 0:NV], T.vels[:, 0:NV], ["vels"], ["velb"])
    ghosts(1)
    op("V", lambda: V.memset(T.one[:, 128:HB], 1.0), [], ["one1"])

    def whole(out, f, base, r, w):
        op("V", lambda: V.tensor_scalar(out, fld(BX, f), RND + base, -RND, A.add, A.add), r, pb(BX) + w)

    whole(zf(T.ZS, SB - 1), 0, NO, ["ZS"], ["z3"])
    op("P", tolist(BW, 0, T.ZS, SB - 1, True, True), ["z3", "ZS"], pb(BW))
    whole(zf(T.ZS, PA - 1), 1, NI, ["ZS"], ["z4"])
    cast(SB, 1, BW)
    vs(T.Bn[:], T.Bp[:], -1.0, A.mult, ["Bp"], ["Bn"])
    op("V", lambda: V.tensor_scalar(ub(IDB), T.iv[0:UP], 2.0, 1.0, A.mult, A.add), ["iv", "UB"], ["u6"])
    vc(ub(SB), zf(T.ZS, SB - 1), ["z3", "UB"], ["u3"])
    vc(ub(PA), zf(T.ZS, PA - 1), ["z4", "UB"], ["u4"])
    vt(zf(T.ZS, IC - 1), ub(KL), ub(KR), A.min, ["u1", "u2", "ZS"], ["z5"])
    op("V", lambda: V.tensor_reduce(T.bias[:, 0:1], T.bt[:, 8:16], AxisListType.X, A.add, negate=True), ["bt1"], ["bias0"])
    op("V", lambda: V.tensor_reduce(T.bt[:, 25:26], T.bt[:, 16:24], AxisListType.X, A.add), ["bt2"], ["bt4"])

    def zcopy(t):
        twin(zf(T.ZS, t - 1), ub(t), 64, ["u%d" % t, "ZS"], ["z%d" % t])

    send(1)
    fill(T.T0[:, 0:SH], SH, 0, [], ["T0t"])
    fill(T.T0[:, NI:904], 8, -4096, [], ["T0t"])
    fill(T.KK[:, 0:SH], SH, 0, [], ["KKp"])
    fill(T.KK[:, SH + NI:912], 912 - SH - NI, 0, [], ["KKp"])
    fill(T.rows[:], 64, -1, [], ["rows"])
    put(T.nb[:], T.zero[:, 0:64], [[0, 8]] + G8, 0, -1.0, ["zero"], ["nb"])
    op("G", lambda: g.iota(T.iv2[:], [[0, 8], [-1, 2], [2, 8]], 1, 16, allow_small_or_imprecise_dtypes=True), [], ["iv2"])
    put(T.sK[:, 0:32], T.nb[:, 0:32], [[0, 4]] + G8, IDB, 1.0, ["nb"], ["sK"])
    put(T.sK[:, 32:64], T.nb[:, 0:32], [[0, 2], [-1, 2]] + G8, KL, 1.0, ["nb"], ["sK"])
    put(T.sGn[:, 0:32], T.zero[:, 0:32], [[0, 4]] + G8, PA, -4096.0, ["zero"], ["sGa"])
    put(T.sGn[:, 32:48], T.zero[:, 0:16], G8 + [[0, 2]], PA, -4096.0, ["zero"], ["sGb"])
    put(T.nb2[:], T.zero[:, 0:16], G8 + [[0, 2]], 0, -1.0, ["zero"], ["nb2"])
    put(T.sP[:, 0:16], T.nb[:, 0:16], [[0, 2]] + G8, IDB, 1.0, ["nb"], ["sP"])
    fill(T.sP[:, 32:48], 16, 0, [], ["sP"])
    put(T.sP[:, 16:32], T.nb2[:], G8 + [[0, 2]], IDB, 1.0, ["nb2"], ["sP"])
    put(T.sP[:, 48:64], T.nb[:, 0:16], [[1, 2]] + G8, KR, 1.0, ["nb"], ["sP"])
    for k in (T.UPT, T.UU):
        fill(k[:, 0:SH], SH, 0, [], ["UPp"])
        fill(k[:, NI:912], 912 - NI, 0, [], ["UPp"])
    zcopy(KL)
    zcopy(KR)

    def last_fills():
        fill(T.NT[:, 0:SH], SH, 0, [], ["NTp"])
        fill(T.NT[:, SH + NI:912], 912 - SH - NI, 0, [], ["NTp"])
        put(T.sN[:, 0:16], T.zero[:, 0:16], [[0, 2]] + G8, SB, 1.0, ["zero"], ["sN0"])
        put(T.sN[:, 16:32], T.zero[:, 0:16], [[-1, 2]] + G8, KL, 1.0, ["zero"], ["sN"])
        put(T.sN[:, 32:48], T.zero[:, 0:16], [[1, 2]] + G8, KR, 1.0, ["zero"], ["sN"])
        put(T.sN[:, 48:64], T.zero[:, 0:16], [[0, 2]] + G8, PA, 1.0, ["zero"], ["sN1"])
        put(T.sN[:, 16:48], T.sN[:, 16:48], [[0, 2], [-1, 2]] + G8, MC, -4096.0, ["sN"], ["sN"])
        fill(T.H2[:, NI:NI + SH], SH, 0, [], ["H2q"])
        for k in (1, 2):
            fill(H[k][:, 0:SH], SH, 0, [], ["H%dp" % k])
            fill(H[k][:, TW - 8:TW], 8, 0, [], ["H%dp" % k])

    def gain_start(h):
        op("P", mm(bank(D0 + h, 0, HB), T.crow[0:1], T.one[0:1, :], True, False), ["crow", "one", "one1"], pb(D0 + h))

    def gain_sum(t, h):
        op("P", mm(bank(D0 + h, 0, HB), T.Bp[:], H[t][:, SH + HB * h:SH + HB * h + HB]), ["Bp"] + hkeys(t)[2 * h:3 + 2 * h], pb(D0 + h))

    for h in range(2):
        gain_start(h)
        gain_sum(0, h)
    uk = ["UB", "u1", "u2", "u3", "u4", "u5", "u6", "u7"]
    for t in range(RO):
        last = t == RO - 1
        Ht, hk = H[t], hkeys(t)
        win = Ht[:]
        for c in range(4):
            a, e = CG[c]
            sc(T.AA[:, a:e], win.indirect(lst(SB, a, e)), hk + ["l3"], ["A%d" % c])
            if c == 1 and t > 0:
                sc(T.UB[0:UP, :, SB:PA + 1, :], T.pS[0:UP, :, 0:2, :], ["UB"], pb(BS) + ["u3", "u4"])
        for c in range(4):
            a, e = CG[c]
            h = c // 2
            fb = (F0, F0, F1, BX)[c]
            vt(T.M0[:, a:e], win.indirect(lst(KR, a, e)), T.AA[:, a:e], A.max, hk + ["l2", "A%d" % c], ["M0%d" % c])
            vt(T.M1[:, a:e], win.indirect(lst(KL, a, e)), T.AA[:, a:e], A.max, hk + ["l1", "A%d" % c], ["M1%d" % c])
            if c == 1:
                for j in range(2):
                    op("P", unwrap(j, False), uk, pb(D0 + j))
            op("P", [mm(bank(D0 + h, a - HB * h, e - HB * h), T.Bn[:], T.M0[:, a:e], False, c % 2 == 1),
                     mm(bank(fb, a - HB * h, e - HB * h), T.Bp[:], T.M0[:, a:e], True, False)], ["Bn", "Bp", "M0%d" % c], pb(D0 + h, fb))
            op("P", mm(bank(fb, a - HB * h, e - HB * h), T.Bn[:], T.M1[:, a:e], False, True), ["M1%d" % c], pb(fb))
            if c == 0 and t == 0:
                for f in leaves(1, BY):
                    f()
            if c == 1:
                op("P", tolist(BW, 0, T.ZS, PA - 1, True) + [m for f in range(4 * (t > 0)) for m in tolist(BW, 0, T.ZP, f)] +
                   tolist(BW, 1, T.ZS, IC - 1, False, True), ["z4", "z5", "ZP"], pb(BW))
                if t > 0:
                    zcopy(SB)
                    zcopy(PA)
            if c > 0:
                a = 0 if c == 1 else a
                op("S", lambda: S.activation(T.RR[:, a:e], bank(fb, a - HB * h, e - HB * h), F.Relu, bias=T.bias[:, 0:1]), ["bias0"],
                   pb(fb) + ["RR%d" % c])
        vt(T.T0[:, SH:SH + HB], bank(D0, 0, HB), T.RR[:, 0:HB], A.add, ["RR1", "T0t"], pb(D0) + ["T00"])
        vt(T.T0[:, SH + HB:SH + NI], bank(D1, 0, HB), T.RR[:, HB:NI], A.add, ["RR2", "RR3", "T0t"], pb(D1) + ["T01"])
        cast(PA, 2, BW)
        if t == 0:
            op("S", lambda: S.activation(T.bias[:, 1:2], T.bt[:, 25:26], F.Identity, bias=2048.0, scale=-2048.0), ["bt4"], ["bias1"])
            op("S", lambda: S.activation(T.In1[:], T.Ib[:], F.Identity, scale=-1.0), ["Ib"], ["In1"])
            op("S", lambda: S.activation(T.In2[:], T.Ib[:], F.Identity, scale=-2.0), ["Ib"], ["In2"])
        tk = ["T00", "T01", "T0t", "T0u", "T0v"]
        for c in range(5):
            a, e = CK[c]
            if c == 0:
                op("V", lambda: V.tensor_scalar(T.TT[:, a:e], T.T0[:].indirect(lst(KL, a, e)), T.bias[:, 1:2], 0.0, A.add, A.max),
                   tk + ["l1", "bias1"], ["TT0"])
            else:
                op("S", lambda: S.activation(T.TT[:, a:e], T.T0[:].indirect(lst(KL, a, e)), F.Relu, bias=T.bias[:, 1:2]),
                   tk + ["l1", "bias1"], ["TT%d" % c])
            vt(T.KK[:, SH + a:SH + e], T.T0[:].indirect(lst(KR, a, e)), T.TT[:, a:e], A.max, tk + ["l2", "TT%d" % c], ["KK%d" % c])
            if 0 < c < 4:
                a, e = CU[c - 1]
                twin(T.K2[:, a:e], T.KK[:, SH + a:SH + e], e - a, ["KK0", "KK%d" % c], ["K2%d" % (c - 1)])
        if t == 0:
            sc(T.idc[:], T.iv2[:], ["iv2"], ["idc"])
            op("S", lambda: S.activation(T.sGp[:], T.sGn[:], F.Identity, scale=-1.0), ["sGa", "sGb"], ["sGp"])
        sc(T.K2[:, CU[3][0]:NI], T.KK[:, SH + CU[3][0]:SH + NI], ["KK4"], ["K23"])
        kk, up, uu = names("KK", 5) + ["KKp"], names("UP") + ["UPp", "UPr"], names("UU") + ["UPp", "UPr"]
        op("P", [less1(fld(BX, 0), True), less1(fld(BX, 2))] +
           [mm(fld(BX, f), J2, ub((KL, KL, KR, KR)[f])) for f in range(4)] +
           [mm(fld(BX, 4 + f), J1, ub((KR, KR, KL, KL)[f])) for f in range(4)], ["rows", "In1", "In2", "u1", "u2"], pb(BX))
        if not last:
            op("P", [mm(fld(F0, 6 + f), I1, ub(PA), f == 0) for f in range(2)] + [mm(fld(F0, 6 + f), J1, ub(SB), False, f == 1) for f in range(2)],
               ["u3", "u4"], pb(F0))
            op("P", [mm(fld(F1, f), J1, ub((SB, SB, ID, ID, ID, ID, PA, PA)[f]), f == 0) for f in range(8)], ["u3", "u4", "u5"], pb(F1))
        op("P", tolist(BW, 0, T.ZS, 0, True) + tolist(BW, 1, T.ZS, 1), ["z1", "z2"], pb(BW))
        op("P", [mm(st(j), I1, ub(KL + j), j == 0) for j in range(2)], ["u1", "u2"], pb(BS))
        op("P", wrap(T.KK, SH, T.sK[:], BX, 8), kk + ["sK"], pb(BX))
        op("P", [less1(fld(BY, 0), True), mm(fld(BY, 2, 2), J1, T.idc[0:UP])] +
           [mm(fld(BY, f), (J2, J2, None, None, I1, I1, J1, J1)[f], ub(SB)) for f in (0, 1, 4, 5, 6, 7)] +
           [mm(fld(BY, 4 + f), J1, ub(KL + f)) for f in range(2)], ["u3", "idc"], pb(BY))
        if last:
            lv = leaves(t, D0)
        for c in range(4):
            a, e = CU[c]
            vt(T.UPT[:, SH + a:SH + e], T.KK[:].indirect(lst(PA, a, e)), T.K2[:, a:e], A.is_lt, kk + ["K2%d" % c, "l4", "UPp"], ["UP%d" % c])
            if c < 3:
                twin(T.U2[:, a:e], T.UPT[:, SH + a:SH + e], e - a, ["UP%d" % c], ["U2%d" % c])
        sc(T.KP[:], T.KK[:].indirect(lst(PA)), kk + ["l4"], ["KP"])
        op("P", wrap(T.KP, 0, T.sP[:], BY, 8), ["KP", "sP"], pb(BY))
        op("P", wrap(T.UPT, SH, T.sGn[:, 0:32], BX, 4), up + ["sGa", "sGb"], pb(BX))
        vc(T.U2[:, CU[3][0]:NI], T.UPT[:, SH + CU[3][0]:SH + NI], ["UP3"], ["U23"])
        for c in range(4):
            a, e = CU[c]
            vt(T.UU[:, SH + a:SH + e], T.UPT[:].indirect(lst(SB, a, e)), T.U2[:, a:e], A.max, up + ["U2%d" % c, "l3"], ["UU%d" % c])
        sc(T.DD[:], T.UPT[:].indirect(lst(PA)), up + ["l4"], ["DD"])
        op("P", wrap(T.DD, 0, T.sGn[:, 16:48], BY, 4), ["DD"], pb(BY))
        op("P", wrap(T.UU, SH, T.sGp[:, 16:48], BY, 4, True), uu + ["sGp"], pb(BY))
        nv = N1V if last else N1A
        vc(T.N1[:, 0:nv], T.UU[:].indirect(lst(IC, 0, nv)), uu + ["l5"], ["N10"])
        sc(T.N1[:, N1V:NI], T.UU[:].indirect(lst(IC, N1V, NI)), uu + ["l5"], ["N11"])
        if t == 0:
            last_fills()
        if last:
            for f in lv:
                f()
            dma("Y", "o0", [(T.yh[:, NI:NI + NV], T.H3[:, NI:NI + NV])], ["H3l"], [])
        vs(T.UB[0:UP, :, MC:MD + 1, :], fld(BY, 2, 2), -4096.0, A.is_equal, ["UB"], pb(BY) + ["u7"])
        if not last:
            op("P", unwrap(0, True), uk, pb(D0))
            vc(T.N1[:, nv:N1V], T.UU[:].indirect(lst(IC, nv, N1V)), uu + ["l5"], ["N12"])
        op("P", wrap(T.N1, 0, T.sGp[:, 0:32], BX, 4, True), ["N10", "N11", "N12"], pb(BX))
        for f in range(2):
            vt(zf(T.ZY, 2 + f), fld(BY, 4 + f), ub(MC + f), A.mult, ["u7", "ZY"], pb(BY) + ["ZYu"])
        if not last:
            op("P", unwrap(1, True), uk, pb(D1))
            vs(T.MK[0:UP, 2, :], fld(BY, 0, 2), -4096.0, A.is_equal, [], pb(BY) + ["MK1"])
            for h in range(2):
                sc(T.NT[:, SH + HB * h:SH + HB * h + HB], bank(D0 + h, 0, HB), [], pb(D0 + h) + ["NT%d" % h])
        op("P", [m for f in range(2) for m in tolist(BW, f, T.ZY, 2 + f)], ["ZYu"], pb(BW))
        op("P", [mm(st(f), I1, zf(T.ZY, 2 + f)) for f in range(2)], ["ZYu"], pb(BS))
        vs(T.EQ[0:UP], fld(BX, 0, 4), -4096.0, A.is_equal, [], pb(BX) + ["EQ"])
        vt(zf(T.ZX, 0, 4), fld(BX, 4, 4), T.EQ[0:UP], A.mult, ["EQ", "ZX"], pb(BX) + ["ZX"])
        op("P", [m for f in range(4) for m in tolist(BW, 1 - f // 2, T.ZX, f, False, f == 3)], ["ZX"], pb(BW))
        op("P", [mm(st(1 - f // 2), I1, zf(T.ZX, f), False, f == 3) for f in range(4)], ["ZX"], pb(BS))
        if not last:
            vt(zf(T.ZY, 0, 2), fld(BY, 6, 2), T.MK[0:UP, 2, :], A.mult, ["MK1", "ZY"], pb(BY) + ["ZYw"])
        vs(T.lst[:, 0:2, :], bank(BW, 0, 112), SH, A.add, [], pb(BW) + ["l1", "l2"])

        CN = CO if last else CK

        def newc(c):
            a, e = CN[c]
            (sc if c else vc)(T.BB[:, a:e], win.indirect(lst(KL, a, e)), hk + ["l1"], ["B%d" % c])

        def newm(c):
            a, e = CN[c]
            out = T.H3[:, a:e] if last else H[t + 1][:, SH + a:SH + e]
            vt(out, win.indirect(lst(KR, a, e)), T.BB[:, a:e], A.max, hk + ["l2", "B%d" % c], ["H%d_%d" % (t + 1, c)] + ["H%dq" % (t + 1)] * (c == 4))

        if not last:
            nt = ["NT0", "NT1", "NTp", "l4"]
            sc(T.NP[:, 0:NPS], T.NT[:].indirect(lst(PA, 0, NPS)), nt, ["NP0"])
            vc(T.NP[:, NPS:NI], T.NT[:].indirect(lst(PA, NPS, NI)), nt, ["NP1"])
            op("P", tolist(BX, 0, T.ZS, SB - 1, True) + [m for f in range(4) for m in tolist(BX, 0, T.ZY, f, eye=T.Ih if f < 2 else T.In1)],
               ["z3", "ZYu", "ZYw"], pb(BX))
            op("P", [mm(fld(BW, f), I1, ub(SB), f == 0) for f in range(2)] + [mm(fld(BW, f), J1, ub(PA), False, f == 1) for f in range(2)],
               ["u3", "u4"], pb(BW))
            op("P", wrap(T.NP, 0, T.sN[:], F1, 8, True), ["NP0", "NP1", "sN", "sN0", "sN1"], pb(F1))
            for h in range(2):
                gain_start(h)
            for c in range(5):
                newc(c)
            sc(T.UB[0:UP, :, KL:KR + 1, :], T.pS[0:UP, :, 0:2, :], ["UB"], pb(BS) + ["u1", "u2"])
            zcopy(KL)
            zcopy(KR)
            newm(0)
            newm(1)
            vs(T.MK[0:UP, 0:2, :], fld(F1, 2, 4), -4096.0, A.is_equal, [], pb(F1) + ["MK0"])
            newm(2)
            vt(zf(T.ZX, 0, 4), fld(F0, 6, 4), T.MK[0:UP, 0:2, :], A.mult, ["MK0", "ZX"], pb(F0, F1) + ["ZX"])
            op("P", [m for f in range(4) for m in tolist(BX, 0, T.ZX, f, False, f == 3)], ["ZX"], pb(BX))
            newm(3)
            newm(4)
            if t == 0:
                ghosts(2)
                send(2)
            cast(SB, 1, BX)
            op("P", [mm(st(j), I1, ub(SB + j), j == 0) for j in range(2)] + [mm(st(0), I1 if f < 2 else J1, zf(T.ZY, f)) for f in range(4)] +
               [mm(st(0), I1, zf(T.ZX, f)) for f in range(4)], ["u3", "u4", "ZYu", "ZYw", "ZX"], pb(BS))
            for h in range(2):
                gain_sum(t + 1, h)
            vt(zf(T.ZP, 0, 4), fld(F1, 6, 4), T.MK[0:UP, 0:3:2, :], A.mult, ["MK0", "MK1", "ZP"], pb(F1, BW) + ["ZP"])
            vt(zf(T.ZS, IC - 1), ub(KL), ub(KR), A.min, ["u1", "u2", "ZS"], ["z5"])
            op("P", [mm(st(1), I1, zf(T.ZP, f), False, f == 3) for f in range(4)], ["ZP"], pb(BS))
        else:
            newc(0)
            vc(T.UK[0:UP, 16:144:8, :], T.pS[0:UP, :, 0:2, :], ["UK"], pb(BS) + ["uk"])
            op("P", [mm(T.PS[:, 512 * F0 + r:512 * F0 + 224:8], T.UK[0:UP, 16 - 2 * j:144 - 2 * j, r], T.Ih[0:UP, 28 * j:28 * j + 28],
                        r + j == 0, r + j == 10) for r in range(8) for j in range(4)], ["uk", "UK"], pb(F0))
            for c in range(5):
                a, e = CN[c]
                if c > 0:
                    newc(c)
                newm(c)
                if c > 0:
                    a = 0 if c == 1 else a
                    dma("Y", "o%d" % c, [(T.yh[:, a:e], T.H3[:, a:e])], ["H3_0", "H3_%d" % c], [])
            sc(T.NK[:], bank(F0, 0, 224), [], pb(F0) + ["NK"])
            dma("S", "o5", [(T.yk[:], T.NK[0:128:2, :])], ["NK"], [])

    for s in top:
        need("G", (s, top[s]))
